import numpy as np
import ml_dtypes


def mxq(x, axis, fmt="e4m3"):
    dtype, down = {"e4m3": (ml_dtypes.float8_e4m3fn, 7), "e5m2": (ml_dtypes.float8_e5m2, 14)}[fmt]
    v = np.moveaxis(np.asarray(x, np.float32).astype(ml_dtypes.bfloat16).astype(np.float64), axis, -1)
    blocks = v.reshape(v.shape[:-1] + (-1, 32))
    amax = np.abs(blocks).max(-1, keepdims=True)
    byte = np.maximum(np.where(amax > 0, np.frexp(amax)[1] - 1 + 127, 0) - down, 1)
    scale = np.exp2(byte - 127.0)
    codes = (blocks / scale).astype(np.float32).astype(dtype).astype(np.float64)
    return np.moveaxis((codes * scale).reshape(v.shape), -1, axis)


WIDE = False


def mx_kscale(k):
    if not WIDE:
        return np.ones(k)
    levels = np.array([24, -24, 12, -12, 0])
    if k % 512:
        return np.exp2(np.random.permutation(np.resize(levels, k // 32))).repeat(32)
    a = np.empty((k // 512, 16))
    for p in range(k // 512):
        a[p, :8] = np.random.permutation(np.resize(levels, 8))
        for g in range(8):
            far = levels[np.abs(levels - a[p, g]) >= 10]
            a[p, g + 8] = far[np.random.randint(len(far))]
    return np.exp2(a.ravel()).repeat(32)


def f64(x):
    return np.asarray(x).astype(np.float64)


def striped(idx):
    return np.tile(idx.reshape(-1, 16).T, (8, 1)).astype(np.uint16)


def unstriped(offs):
    return offs[:16].T.reshape(-1).astype(np.int64)


E2M1 = np.array([0.0, 0.5, 1.0, 1.5, 2.0, 3.0, 4.0, 6.0, -0.0, -0.5, -1.0, -1.5, -2.0, -3.0, -4.0, -6.0])


def pack_weight(w, fmt):
    k, n = w.shape
    w = f64(np.asarray(w, np.float32).astype(ml_dtypes.bfloat16)).reshape(k // 32, 32, n)
    amax = np.abs(w).max(1)
    if fmt == "e4m3":
        byte = np.frexp(amax)[1] - 1 + 127 - 7
    else:
        mant, ex = np.frexp(amax / 6.0)
        byte = np.where(mant > 0.5, ex, ex - 1) + 127
    byte = np.clip(np.where(amax > 0, byte, 1), 1, 254)
    scaled = (w * np.exp2(127.0 - byte)[:, None, :]).reshape(k, n).astype(np.float32)
    by_word = np.ascontiguousarray(scaled.reshape(k // 512, 128, 4, n).transpose(0, 1, 3, 2))
    if fmt == "e4m3":
        words = by_word.astype(ml_dtypes.float8_e4m3fn).view(np.uint8)
    else:
        c = by_word.astype(ml_dtypes.float4_e2m1fn).view(np.uint8) & 0xF
        words = (c[..., 0::2] | (c[..., 1::2] << 4)).reshape(k // 512, 128, 2 * n)
    return np.ascontiguousarray(words), np.ascontiguousarray(byte.astype(np.uint8).reshape(k // 512, 16, n))


def unpack_weight(words, scales, fmt):
    g, _, n = scales.shape
    words = np.ascontiguousarray(words).reshape(g, 128, n, -1)
    if fmt == "e4m3":
        vals = words.view(ml_dtypes.float8_e4m3fn).astype(np.float64)
    else:
        nib = np.empty((g, 128, n, 4), np.uint8)
        nib[..., 0::2] = words & 0xF
        nib[..., 1::2] = words >> 4
        vals = E2M1[nib]
    vals = vals * np.repeat(np.exp2(scales.astype(np.float64) - 127.0), 8, axis=1)[..., None]
    return vals.transpose(0, 1, 3, 2).reshape(g * 512, n)


def pack_table4(v):
    words, scales = pack_weight(v, "e2m1")
    g, t = words.shape[0] // 2, v.shape[1]
    return np.ascontiguousarray(words.reshape(g, 2, 128, t, 2).transpose(0, 2, 3, 1, 4).reshape(g, 128, t, 4)), scales


def unpack_table4(words, scales):
    g, _, t, _ = words.shape
    return unpack_weight(words.reshape(g, 128, t, 2, 2).transpose(0, 3, 1, 2, 4).reshape(2 * g, 128, 2 * t), scales, "e2m1")


def planes(y):
    n, m = y.shape
    v = y.astype(np.float32).astype(ml_dtypes.bfloat16).astype(np.float64).reshape(n // 32, 32, m)
    top = np.abs(v).max(1)
    byte = np.clip(np.where(top > 0, np.frexp(top)[1] - 1 + 127 - 7, 1), 1, 254)
    codes = (v * np.exp2(127.0 - byte)[:, None, :]).reshape(n, m).astype(np.float32).astype(ml_dtypes.float8_e4m3fn).view(np.uint8)
    words = codes.reshape(n // 512, 128, 4, m).transpose(0, 1, 3, 2)
    return np.ascontiguousarray(words), np.ascontiguousarray(byte.astype(np.uint8).reshape(n // 512, 16, m))


def silu(f):
    return f / (1.0 + np.exp(-np.maximum(f, -700.0)))


def sigm(f):
    return 1.0 / (1.0 + np.exp(-np.maximum(f, -700.0)))


K, N, T, J = 1024, 512, 2048, 1024


def setup_inputs():
    n = np.random.standard_normal
    s = mx_kscale(K)[:, None]
    p_tab = pack_table4(n((K, T)) * s)
    p_wa = pack_weight(n((K, N)) / np.sqrt(2 * K) / s, "e2m1")
    p_wb = pack_weight(n((K, N)) / np.sqrt(2 * K) / s, "e4m3")
    p_wo = pack_weight(n((K, N)) / np.sqrt(K) / s, "e2m1")
    return {
        "tab_words": p_tab[0],
        "tab_scales": p_tab[1],
        "wa_words": p_wa[0],
        "wa_scales": p_wa[1],
        "wb_words": p_wb[0],
        "wb_scales": p_wb[1],
        "wc": (n((K, N)) / np.sqrt(K) / s).astype(np.float32),
        "wo_words": p_wo[0],
        "wo_scales": p_wo[1],
        "b": (0.3 * n(N)).astype(np.float32),
        "wgo": np.tile(np.random.uniform(0.5, 2.0, J), (128, 1)).astype(np.float32),
        "offs": striped(np.random.permutation(T)[:J]),
        "offs2": striped(np.random.permutation(T)[:J]),
    }


def reference(tab_words, tab_scales, wa_words, wa_scales, wb_words, wb_scales, wc, wo_words, wo_scales, b, wgo, offs, offs2):
    idx = unstriped(offs)
    idx2 = unstriped(offs2)
    tab_ = unpack_table4(tab_words, tab_scales)[:, idx]
    tabb_ = unpack_table4(tab_words, tab_scales)[:, idx2]
    wa_ = unpack_weight(wa_words, wa_scales, "e2m1")
    wb_ = unpack_weight(wb_words, wb_scales, "e4m3")
    za = wa_.T @ tabb_ + wb_.T @ tab_
    eta = sigm(za)
    wc_ = mxq(f64(wc), 0, "e4m3")
    ms = wc_.T @ tab_
    wo_ = unpack_weight(wo_words, wo_scales, "e2m1")
    ow = wo_.T @ tabb_
    out = np.zeros((N, T))
    out[:, idx2] = f64(wgo)[0] * (silu(ow + eta * ms + f64(b)[:, None]))
    return (out,) + planes(out)

@@ -1,0 +1,230 @@
+from contextlib import ExitStack
+
+import concourse.mybir as mybir
+from concourse.masks import make_identity
+
+K, N, T, J = 1024, 512, 2048, 1024
+FLOPS = 4 * 2 * K * N * J
+
+F32 = mybir.dt.float32
+BF16 = mybir.dt.bfloat16
+I32 = mybir.dt.int32
+U32 = mybir.dt.uint32
+U16 = mybir.dt.uint16
+U8 = mybir.dt.uint8
+FP8X4 = mybir.dt.float8_e4m3fn_x4
+FP4X4 = mybir.dt.float4_e2m1fn_x4
+ACT = mybir.ActivationFunctionType
+ALU = mybir.AluOpType
+
+P = 128
+PASSES = 2
+EDGE_TILES = J // P
+GATHER_PIECES = (256, 256, 512)
+CHUNK = 256
+SRC, DST = 0, 1
+SCATTER_RUNS = (
+    ((0, 2), (2, 4), (4, 6), (6, 8)),
+    ((0, 2), (2, 4), (4, 6), (6, 8)),
+    ((0, 3), (3, 5), (5, 8)),
+    ((0, 3), (3, 8)),
+)
+
+
+def tile_list_rgg_ownsiluP_kernel(tc, tab_words, tab_scales, wa_words, wa_scales, wb_words, wb_scales, wc,
+        wo_words, wo_scales, b, wgo, offs, offs2, out_0, out_1, out_2):
+    nc = tc.nc
+    with ExitStack() as ctx:
+        keep = ctx.enter_context(tc.tile_pool(name="keep", bufs=1))
+        ring = ctx.enter_context(tc.tile_pool(name="ring", bufs=3))
+        psum = ctx.enter_context(tc.psum_pool(name="psum", bufs=2))
+
+        lists = [keep.tile([P, J // 16], U16, name="list_src"), keep.tile([P, J // 16], U16, name="list_dst")]
+        tab_sc = keep.tile([P, T], U8, align_bytes=64)
+        nc.vector.memset(tab_sc[:].bitcast(I32), 0)
+        nc.sync.dma_start(lists[DST][:], offs2)
+        nc.sync.dma_start(lists[SRC][:], offs)
+        for q in range(4):
+            nc.sync.dma_start(tab_sc[32 * q : 32 * q + 8, :].bitcast(I32), tab_scales[:, 4 * q : 4 * q + 4, :].bitcast(I32))
+        tab_w = keep.tile([P, T], I32, align_bytes=64)
+        nc.sync.dma_start(tab_w[:], tab_words[0].rearrange("p t i -> p (t i)").bitcast(I32))
+
+        w_sc_rows = keep.tile([16, 3, PASSES, N], U8, align_bytes=64)
+        for w, scales in enumerate((wa_scales, wb_scales, wo_scales)):
+            nc.gpsimd.dma_start(w_sc_rows[:, w].bitcast(I32), scales.rearrange("a q n -> q a n").bitcast(I32))
+        w_sc = keep.tile([P, 3, PASSES, N], U8, align_bytes=64)
+        nc.gpsimd.memset(w_sc[:].rearrange("p w a n -> p (w a n)").bitcast(I32), 0)
+        for q in range(4):
+            nc.gpsimd.dma_start(w_sc[32 * q : 32 * q + 4].rearrange("p w a n -> p (w a n)").bitcast(I32),
+                                w_sc_rows[4 * q : 4 * q + 4].rearrange("p w a n -> p (w a n)").bitcast(I32))
+
+        wc_raw = [keep.tile([P, 4, N], F32, name="wc_raw%d" % a) for a in range(PASSES)]
+        for a in range(PASSES):
+            nc.sync.dma_start(wc_raw[a][:], wc[512 * a : 512 * (a + 1), :].rearrange("(p i) n -> p i n", i=4))
+        wa_w = keep.tile([P, PASSES, 2 * N], U8, align_bytes=64)
+        nc.sync.dma_start(wa_w[:].bitcast(I32), wa_words.rearrange("a p c -> p a c").bitcast(I32))
+        wb_w = keep.tile([P, PASSES, N], I32, align_bytes=64)
+        nc.sync.dma_start(wb_w[:], wb_words.rearrange("a p n i -> p a (n i)").bitcast(I32))
+        wo_w = keep.tile([P, PASSES, 2 * N], U8, align_bytes=64)
+        nc.sync.dma_start(wo_w[:].bitcast(I32), wo_words.rearrange("a p c -> p a c").bitcast(I32))
+
+        ident = keep.tile([P, P], F32)
+        make_identity(nc, ident[:])
+
+        got_sc = keep.tile([P, 2, J], U8, align_bytes=64)
+        got_sc1 = keep.tile([P, 2, J], U8, align_bytes=64)
+        nc.gpsimd.memset(got_sc1[:].rearrange("p l j -> p (l j)").bitcast(I32), 0)
+        pages = [keep.tile([P, T], F32, name="page%d" % t) for t in range(4)]
+        for t in range(4):
+            for c in range(0, T, 512):
+                if t < 2:
+                    nc.vector.memset(pages[t][:, c : c + 512], 0.0)
+                else:
+                    nc.gpsimd.memset(pages[t][:, c : c + 512], 0.0)
+
+        for side in (DST, SRC):
+            nc.vector.tensor_copy(got_sc[:, side, :], tab_sc[:].indirect(lists[side][:]))
+        for q in range(4):
+            nc.sync.dma_start(got_sc1[32 * q : 32 * q + 4].rearrange("p l j -> p (l j)").bitcast(I32),
+                              got_sc[32 * q + 4 : 32 * q + 8].rearrange("p l j -> p (l j)").bitcast(I32))
+        bias = keep.tile([P, 4], F32)
+        nc.sync.dma_start(bias[:], b.rearrange("(p t) -> p t", t=4))
+        gate_w = keep.tile([P, J], F32)
+        nc.sync.dma_start(gate_w[:], wgo)
+        node_sc = (got_sc, got_sc1)
+
+        wc_w = keep.tile([P, PASSES, N], U32, align_bytes=64)
+        wc_sc = keep.tile([P, PASSES, N], U8, align_bytes=64)
+        wc_bf = [keep.tile([P, N, 4], BF16, align_bytes=64, name="wc_bf%d" % a) for a in range(PASSES)]
+        for a in range(PASSES):
+            nc.scalar.copy(wc_bf[a][:].rearrange("p (c e) i -> p c i e", e=4), wc_raw[a][:].rearrange("p i (c e) -> p c i e", e=4))
+
+        def quantise_wc(a):
+            nc.vector.quantize_mx(wc_w[:, a, :].bitcast(FP8X4), wc_sc[:, a, :], wc_bf[a][:].rearrange("p n i -> p (n i)"))
+
+        node_w = {}
+        first = 0
+        for piece, width in enumerate(GATHER_PIECES):
+            got_w = keep.tile([P, 2, width], U32, align_bytes=64, name="got_w%d" % piece)
+            for side in (DST, SRC):
+                nc.vector.tensor_copy(got_w[:, side, :],
+                                      tab_w[:].bitcast(U32).indirect(lists[side][:, first // 16 : (first + width) // 16]))
+            parted = keep.tile([P, 2, PASSES, 2 * width], U8, align_bytes=64, name="parted%d" % piece)
+            nc.vector.tensor_copy(parted[:].bitcast(U16), got_w[:].bitcast(U16).rearrange("p l (j a) -> p l a j", a=2))
+            for j in range(first // P, (first + width) // P):
+                node_w[j] = (parted, j * P - first)
+            first = first + width
+            if piece < PASSES:
+                quantise_wc(piece)
+
+        acts = [keep.tile([P, J], F32, name="act%d" % t) for t in range(4)]
+        terms = {}
+
+        def product(acc, j, side, a, w, w_scale, start, stop):
+            parted, col = node_w[j]
+            nc.tensor.matmul_mx(acc[:], lhsT=parted[:, side, a, 2 * col : 2 * col + 2 * P].bitcast(FP4X4),
+                                lhsT_scale=node_sc[a][:, side, j * P : (j + 1) * P],
+                                rhs=w, rhs_scale=w_scale, start=start, stop=stop)
+
+        def dealt(ap):
+            return ap.rearrange("p (m t) -> p t m", t=4)
+
+        def multiply(j):
+            za = psum.tile([P, N], F32)
+            ow = psum.tile([P, N], F32)
+            ms = psum.tile([P, N], F32)
+            for a in range(PASSES):
+                product(za, j, DST, a, wa_w[:, a, :].bitcast(FP4X4), w_sc[:, 0, a, :], a == 0, False)
+            for a in range(PASSES):
+                product(za, j, SRC, a, wb_w[:, a, :].bitcast(FP8X4), w_sc[:, 1, a, :], False, a == PASSES - 1)
+            for a in range(PASSES):
+                product(ow, j, DST, a, wo_w[:, a, :].bitcast(FP4X4), w_sc[:, 2, a, :], a == 0, a == PASSES - 1)
+            for a in range(PASSES):
+                product(ms, j, SRC, a, wc_w[:, a, :].bitcast(FP8X4), wc_sc[:, a, :], a == 0, a == PASSES - 1)
+            th = ring.tile([P, 4, P], F32)
+            nc.scalar.activation(th[:], dealt(za[:]), ACT.Tanh, scale=0.5)
+            own2 = ring.tile([P, 4, P], F32)
+            nc.scalar.activation(own2[:], dealt(ow[:]), ACT.Copy, scale=2.0)
+            msg2 = ring.tile([P, 4, P], F32)
+            nc.vector.scalar_tensor_tensor(msg2[:], th[:], 1.0, dealt(ms[:]), ALU.add, ALU.mult)
+            terms[j] = (own2, msg2)
+
+        def round_page(t, chunk, engine):
+            cols = slice(chunk * CHUNK, (chunk + 1) * CHUNK)
+            dst = pairs[chunk][:, t // 2, :, t % 2]
+            if engine == "scalar":
+                nc.scalar.copy(dst, pages[t][:, cols])
+            else:
+                nc.vector.tensor_copy(dst, pages[t][:, cols])
+
+        def turn(j):
+            own2, msg2 = terms[j]
+            turned = psum.tile([P, 4, P], F32)
+            for t in range(4):
+                nc.tensor.matmul(turned[:, t, :], lhsT=own2[:, t, :], rhs=ident[:], start=True, stop=False, is_transpose=True)
+                nc.tensor.matmul(turned[:, t, :], lhsT=msg2[:, t, :], rhs=ident[:], start=False, stop=True, is_transpose=True)
+            for t in range(4):
+                nc.scalar.activation(acts[t][:, j * P : (j + 1) * P], turned[:, t, :], ACT.Silu, bias=bias[:, t : t + 1], scale=0.5)
+            for t in range(4):
+                for lo, hi in SCATTER_RUNS[t]:
+                    if hi == j + 1:
+                        cols = slice(lo * P, hi * P)
+                        nc.vector.tensor_tensor(pages[t][:].indirect(lists[DST][:, lo * 8 : hi * 8]),
+                                                acts[t][:, cols], gate_w[:, cols], ALU.mult)
+
+        pairs = [keep.tile([P, 2, CHUNK, 2], BF16, align_bytes=64, name="pairs%d" % c) for c in range(T // CHUNK)]
+        multiply(0)
+        for j in range(1, 5):
+            multiply(j)
+            if j < 4:
+                turn(j - 1)
+        for j in range(5, EDGE_TILES):
+            multiply(j)
+            turn(j - 2)
+        turn(EDGE_TILES - 2)
+        turn(EDGE_TILES - 1)
+
+        out_rows = out_0.rearrange("(p t) c -> p t c", t=4)
+        for t in range(4):
+            nc.sync.dma_start(out_rows[:, t, :], pages[t][:])
+        for t in range(3):
+            for chunk in range(T // CHUNK):
+                if t < 2 or chunk % 2 == 1:
+                    round_page(t, chunk, "scalar")
+
+        codes = keep.tile([P, T], U32, align_bytes=64)
+        code_sc = keep.tile([P, T], U8, align_bytes=64)
+        out_words = out_1[0].rearrange("p t i -> p (t i)").bitcast(I32)
+        woven = {}
+
+        def weave(chunk, engine):
+            if engine == "vector":
+                round_page(2, chunk, engine)
+            round_page(3, chunk, engine)
+            tile = keep.tile([P, CHUNK, 4], BF16, align_bytes=64, name="woven%d" % chunk)
+            src = pairs[chunk][:].rearrange("p h c e -> p h (c e)").bitcast(F32).rearrange("p h c -> p c h")
+            dst = tile[:].bitcast(F32)
+            if engine == "scalar":
+                nc.scalar.copy(dst, src)
+            else:
+                nc.vector.tensor_copy(dst, src)
+            woven[chunk] = tile
+
+        def quantise(chunk):
+            cols = slice(chunk * CHUNK, (chunk + 1) * CHUNK)
+            nc.vector.quantize_mx(codes[:, cols].bitcast(FP8X4), code_sc[:, cols], woven[chunk][:].rearrange("p c i -> p (c i)"))
+
+        for pair in range(T // CHUNK // 2):
+            weave(2 * pair, "vector")
+            weave(2 * pair + 1, "scalar")
+            if pair > 0:
+                quantise(2 * pair - 1)
+            quantise(2 * pair)
+            if pair > 0:
+                cols = slice((2 * pair - 2) * CHUNK, 2 * pair * CHUNK)
+                nc.sync.dma_start(out_words[:, cols], codes[:, cols].bitcast(I32))
+        quantise(T // CHUNK - 1)
+        cols = slice(T - 2 * CHUNK, T)
+        nc.sync.dma_start(out_words[:, cols], codes[:, cols].bitcast(I32))
+        for q in range(4):
+            nc.scalar.dma_start(out_2[0, 4 * q : 4 * q + 4, :].bitcast(I32), code_sc[32 * q : 32 * q + 4, :].bitcast(I32))

@@ -20,8 +20,9 @@ ALU = mybir.AluOpType
 P = 128
 PASSES = 2
 EDGE_TILES = J // P
-GATHER_PIECES = (256, 256, 512)
-CHUNK = 256
+PIECE = 256
+VECTOR_CHUNKS = ((0, 512), (512, 1024))
+SCALAR_CHUNKS = ((1024, 1280), (1280, 1536), (1536, 1792), (1792, 2048))
 SRC, DST = 0, 1
 SCATTER_RUNS = (
     ((0, 2), (2, 4), (4, 6), (6, 8)),
@@ -40,8 +41,8 @@ def tile_list_rgg_ownsiluP_kernel(tc, tab_words, tab_scales, wa_words, wa_scales
         psum = ctx.enter_context(tc.psum_pool(name="psum", bufs=2))
 
         lists = [keep.tile([P, J // 16], U16, name="list_src"), keep.tile([P, J // 16], U16, name="list_dst")]
-        tab_sc = keep.tile([P, T], U8, align_bytes=64)
-        nc.vector.memset(tab_sc[:].bitcast(I32), 0)
+        tab_sc = keep.tile([P, T], U8, align_bytes=64, tag="early_late")
+        nc.gpsimd.memset(tab_sc[:].bitcast(I32), 0)
         nc.sync.dma_start(lists[DST][:], offs2)
         nc.sync.dma_start(lists[SRC][:], offs)
         for q in range(4):
@@ -49,73 +50,81 @@ def tile_list_rgg_ownsiluP_kernel(tc, tab_words, tab_scales, wa_words, wa_scales
         tab_w = keep.tile([P, T], I32, align_bytes=64)
         nc.sync.dma_start(tab_w[:], tab_words[0].rearrange("p t i -> p (t i)").bitcast(I32))
 
-        w_sc_rows = keep.tile([16, 3, PASSES, N], U8, align_bytes=64)
-        for w, scales in enumerate((wa_scales, wb_scales, wo_scales)):
-            nc.gpsimd.dma_start(w_sc_rows[:, w].bitcast(I32), scales.rearrange("a q n -> q a n").bitcast(I32))
-        w_sc = keep.tile([P, 3, PASSES, N], U8, align_bytes=64)
-        nc.gpsimd.memset(w_sc[:].rearrange("p w a n -> p (w a n)").bitcast(I32), 0)
-        for q in range(4):
-            nc.gpsimd.dma_start(w_sc[32 * q : 32 * q + 4].rearrange("p w a n -> p (w a n)").bitcast(I32),
-                                w_sc_rows[4 * q : 4 * q + 4].rearrange("p w a n -> p (w a n)").bitcast(I32))
+        w_sc = {}
+        for name in ("wa", "wb", "wo"):
+            w_sc[name] = keep.tile([P, PASSES, N], U8, align_bytes=64, name=name + "_sc")
+            nc.gpsimd.memset(w_sc[name][:].rearrange("p a n -> p (a n)").bitcast(I32), 0)
 
-        wc_raw = [keep.tile([P, 4, N], F32, name="wc_raw%d" % a) for a in range(PASSES)]
-        for a in range(PASSES):
-            nc.sync.dma_start(wc_raw[a][:], wc[512 * a : 512 * (a + 1), :].rearrange("(p i) n -> p i n", i=4))
+        def load_scales(queue, name, scales):
+            for q in range(4):
+                queue.dma_start(w_sc[name][32 * q : 32 * q + 4].bitcast(I32),
+                                scales[:, 4 * q : 4 * q + 4, :].rearrange("a r n -> r a n").bitcast(I32))
+
+        load_scales(nc.gpsimd, "wb", wb_scales)
+        load_scales(nc.gpsimd, "wo", wo_scales)
         wa_w = keep.tile([P, PASSES, 2 * N], U8, align_bytes=64)
         nc.sync.dma_start(wa_w[:].bitcast(I32), wa_words.rearrange("a p c -> p a c").bitcast(I32))
+        load_scales(nc.sync, "wa", wa_scales)
         wb_w = keep.tile([P, PASSES, N], I32, align_bytes=64)
         nc.sync.dma_start(wb_w[:], wb_words.rearrange("a p n i -> p a (n i)").bitcast(I32))
         wo_w = keep.tile([P, PASSES, 2 * N], U8, align_bytes=64)
         nc.sync.dma_start(wo_w[:].bitcast(I32), wo_words.rearrange("a p c -> p a c").bitcast(I32))
+        wc_raw = [keep.tile([P, 4, N], F32, name="wc_raw%d" % a) for a in range(PASSES)]
+        for a in range(PASSES):
+            nc.sync.dma_start(wc_raw[a][:], wc[512 * a : 512 * (a + 1), :].rearrange("(p i) n -> p i n", i=4))
 
         ident = keep.tile([P, P], F32)
         make_identity(nc, ident[:])
 
         got_sc = keep.tile([P, 2, J], U8, align_bytes=64)
         got_sc1 = keep.tile([P, 2, J], U8, align_bytes=64)
-        nc.gpsimd.memset(got_sc1[:].rearrange("p l j -> p (l j)").bitcast(I32), 0)
+        nc.vector.memset(got_sc1[:].rearrange("p l j -> p (l j)").bitcast(I32), 0)
         pages = [keep.tile([P, T], F32, name="page%d" % t) for t in range(4)]
-        for t in range(4):
+        nc.vector.memset(pages[0][:, : T // 2 - 1], 0.0)
+        nc.vector.memset(pages[0][:, T // 2 - 1 :], 0.0)
+        for t in range(1, 4):
             for c in range(0, T, 512):
-                if t < 2:
-                    nc.vector.memset(pages[t][:, c : c + 512], 0.0)
-                else:
-                    nc.gpsimd.memset(pages[t][:, c : c + 512], 0.0)
+                nc.gpsimd.memset(pages[t][:, c : c + 512], 0.0)
 
         for side in (DST, SRC):
             nc.vector.tensor_copy(got_sc[:, side, :], tab_sc[:].indirect(lists[side][:]))
         for q in range(4):
             nc.sync.dma_start(got_sc1[32 * q : 32 * q + 4].rearrange("p l j -> p (l j)").bitcast(I32),
-                              got_sc[32 * q + 4 : 32 * q + 8].rearrange("p l j -> p (l j)").bitcast(I32))
+                                got_sc[32 * q + 4 : 32 * q + 8].rearrange("p l j -> p (l j)").bitcast(I32))
         bias = keep.tile([P, 4], F32)
         nc.sync.dma_start(bias[:], b.rearrange("(p t) -> p t", t=4))
-        gate_w = keep.tile([P, J], F32)
+        gate_w = keep.tile([P, J], F32, align_bytes=64, tag="early_late")
         nc.sync.dma_start(gate_w[:], wgo)
         node_sc = (got_sc, got_sc1)
 
         wc_w = keep.tile([P, PASSES, N], U32, align_bytes=64)
         wc_sc = keep.tile([P, PASSES, N], U8, align_bytes=64)
-        wc_bf = [keep.tile([P, N, 4], BF16, align_bytes=64, name="wc_bf%d" % a) for a in range(PASSES)]
-        for a in range(PASSES):
-            nc.scalar.copy(wc_bf[a][:].rearrange("p (c e) i -> p c i e", e=4), wc_raw[a][:].rearrange("p i (c e) -> p c i e", e=4))
-
-        def quantise_wc(a):
-            nc.vector.quantize_mx(wc_w[:, a, :].bitcast(FP8X4), wc_sc[:, a, :], wc_bf[a][:].rearrange("p n i -> p (n i)"))
-
         node_w = {}
-        first = 0
-        for piece, width in enumerate(GATHER_PIECES):
-            got_w = keep.tile([P, 2, width], U32, align_bytes=64, name="got_w%d" % piece)
+
+        def quantise_wc(a, half):
+            cols = slice(half * N // 2, (half + 1) * N // 2)
+            wc_bf = keep.tile([P, N // 2, 4], BF16, align_bytes=64, name="wc_bf", tag="stage%d" % (2 * a + half))
+            nc.scalar.copy(wc_bf[:].rearrange("p (c e) i -> p c i e", e=4),
+                           wc_raw[a][:, :, cols].rearrange("p i (c e) -> p c i e", e=4))
+            nc.vector.quantize_mx(wc_w[:, a, cols].bitcast(FP8X4), wc_sc[:, a, cols], wc_bf[:].rearrange("p n i -> p (n i)"))
+
+        def gather_words(piece, tag):
+            first = piece * PIECE
+            got_w = keep.tile([P, 2, PIECE], U32, align_bytes=64, name="got_w", tag=tag)
             for side in (DST, SRC):
                 nc.vector.tensor_copy(got_w[:, side, :],
-                                      tab_w[:].bitcast(U32).indirect(lists[side][:, first // 16 : (first + width) // 16]))
-            parted = keep.tile([P, 2, PASSES, 2 * width], U8, align_bytes=64, name="parted%d" % piece)
+                                      tab_w[:].bitcast(U32).indirect(lists[side][:, first // 16 : (first + PIECE) // 16]))
+            parted = keep.tile([P, 2, PASSES, 2 * PIECE], U8, align_bytes=64, name="parted%d" % piece)
             nc.vector.tensor_copy(parted[:].bitcast(U16), got_w[:].bitcast(U16).rearrange("p l (j a) -> p l a j", a=2))
-            for j in range(first // P, (first + width) // P):
+            for j in range(first // P, (first + PIECE) // P):
                 node_w[j] = (parted, j * P - first)
-            first = first + width
-            if piece < PASSES:
-                quantise_wc(piece)
+
+        gather_words(0, "got0")
+        gather_words(1, "got1")
+        for a in range(PASSES):
+            quantise_wc(a, 0)
+            quantise_wc(a, 1)
+            gather_words(2 + a, "stage%d" % (2 * a + 1))
 
         acts = [keep.tile([P, J], F32, name="act%d" % t) for t in range(4)]
         terms = {}
@@ -129,16 +138,22 @@ def tile_list_rgg_ownsiluP_kernel(tc, tab_words, tab_scales, wa_words, wa_scales
         def dealt(ap):
             return ap.rearrange("p (m t) -> p t m", t=4)
 
-        def multiply(j):
-            za = psum.tile([P, N], F32)
-            ow = psum.tile([P, N], F32)
+        sums = {}
+
+        def gate_and_own(j, a):
+            if a == 0:
+                za = psum.tile([P, N], F32)
+                ow = psum.tile([P, N], F32)
+                sums[j] = (za, ow)
+            za, ow = sums[j]
+            last = a == PASSES - 1
+            product(za, j, DST, a, wa_w[:, a, :].bitcast(FP4X4), w_sc["wa"][:, a, :], a == 0, False)
+            product(za, j, SRC, a, wb_w[:, a, :].bitcast(FP8X4), w_sc["wb"][:, a, :], False, last)
+            product(ow, j, DST, a, wo_w[:, a, :].bitcast(FP4X4), w_sc["wo"][:, a, :], a == 0, last)
+
+        def message(j):
+            za, ow = sums[j]
             ms = psum.tile([P, N], F32)
-            for a in range(PASSES):
-                product(za, j, DST, a, wa_w[:, a, :].bitcast(FP4X4), w_sc[:, 0, a, :], a == 0, False)
-            for a in range(PASSES):
-                product(za, j, SRC, a, wb_w[:, a, :].bitcast(FP8X4), w_sc[:, 1, a, :], False, a == PASSES - 1)
-            for a in range(PASSES):
-                product(ow, j, DST, a, wo_w[:, a, :].bitcast(FP4X4), w_sc[:, 2, a, :], a == 0, a == PASSES - 1)
             for a in range(PASSES):
                 product(ms, j, SRC, a, wc_w[:, a, :].bitcast(FP8X4), wc_sc[:, a, :], a == 0, a == PASSES - 1)
             th = ring.tile([P, 4, P], F32)
@@ -149,13 +164,10 @@ def tile_list_rgg_ownsiluP_kernel(tc, tab_words, tab_scales, wa_words, wa_scales
             nc.vector.scalar_tensor_tensor(msg2[:], th[:], 1.0, dealt(ms[:]), ALU.add, ALU.mult)
             terms[j] = (own2, msg2)
 
-        def round_page(t, chunk, engine):
-            cols = slice(chunk * CHUNK, (chunk + 1) * CHUNK)
-            dst = pairs[chunk][:, t // 2, :, t % 2]
-            if engine == "scalar":
-                nc.scalar.copy(dst, pages[t][:, cols])
-            else:
-                nc.vector.tensor_copy(dst, pages[t][:, cols])
+        def multiply(j):
+            for a in range(PASSES):
+                gate_and_own(j, a)
+            message(j)
 
         def turn(j):
             own2, msg2 = terms[j]
@@ -172,9 +184,13 @@ def tile_list_rgg_ownsiluP_kernel(tc, tab_words, tab_scales, wa_words, wa_scales
                         nc.vector.tensor_tensor(pages[t][:].indirect(lists[DST][:, lo * 8 : hi * 8]),
                                                 acts[t][:, cols], gate_w[:, cols], ALU.mult)
 
-        pairs = [keep.tile([P, 2, CHUNK, 2], BF16, align_bytes=64, name="pairs%d" % c) for c in range(T // CHUNK)]
-        multiply(0)
-        for j in range(1, 5):
+        for a in range(PASSES):
+            gate_and_own(0, a)
+            gate_and_own(1, a)
+        message(0)
+        message(1)
+        turn(0)
+        for j in range(2, 5):
             multiply(j)
             if j < 4:
                 turn(j - 1)
@@ -187,44 +203,59 @@ def tile_list_rgg_ownsiluP_kernel(tc, tab_words, tab_scales, wa_words, wa_scales
         out_rows = out_0.rearrange("(p t) c -> p t c", t=4)
         for t in range(4):
             nc.sync.dma_start(out_rows[:, t, :], pages[t][:])
-        for t in range(3):
-            for chunk in range(T // CHUNK):
-                if t < 2 or chunk % 2 == 1:
-                    round_page(t, chunk, "scalar")
 
+        pairs = {}
+        woven = {}
+        for chunk in VECTOR_CHUNKS + SCALAR_CHUNKS:
+            lo, hi = chunk
+            pairs[chunk] = keep.tile([P, 2, hi - lo, 2], BF16, align_bytes=64, name="pairs%d" % lo)
+            woven[chunk] = keep.tile([P, hi - lo, 4], BF16, align_bytes=64, name="woven%d" % lo)
         codes = keep.tile([P, T], U32, align_bytes=64)
         code_sc = keep.tile([P, T], U8, align_bytes=64)
         out_words = out_1[0].rearrange("p t i -> p (t i)").bitcast(I32)
-        woven = {}
 
-        def weave(chunk, engine):
-            if engine == "vector":
-                round_page(2, chunk, engine)
-            round_page(3, chunk, engine)
-            tile = keep.tile([P, CHUNK, 4], BF16, align_bytes=64, name="woven%d" % chunk)
-            src = pairs[chunk][:].rearrange("p h c e -> p h (c e)").bitcast(F32).rearrange("p h c -> p c h")
-            dst = tile[:].bitcast(F32)
-            if engine == "scalar":
-                nc.scalar.copy(dst, src)
-            else:
-                nc.vector.tensor_copy(dst, src)
-            woven[chunk] = tile
+        def round_page(copy, t, chunk):
+            copy(pairs[chunk][:, t // 2, :, t % 2], pages[t][:, chunk[0] : chunk[1]])
+
+        def weave(copy, chunk):
+            words = pairs[chunk][:].rearrange("p h c e -> p h (c e)").bitcast(F32)
+            copy(woven[chunk][:].bitcast(F32), words.rearrange("p h c -> p c h"))
 
         def quantise(chunk):
-            cols = slice(chunk * CHUNK, (chunk + 1) * CHUNK)
+            cols = slice(chunk[0], chunk[1])
             nc.vector.quantize_mx(codes[:, cols].bitcast(FP8X4), code_sc[:, cols], woven[chunk][:].rearrange("p c i -> p (c i)"))
 
-        for pair in range(T // CHUNK // 2):
-            weave(2 * pair, "vector")
-            weave(2 * pair + 1, "scalar")
-            if pair > 0:
-                quantise(2 * pair - 1)
-            quantise(2 * pair)
-            if pair > 0:
-                cols = slice((2 * pair - 2) * CHUNK, 2 * pair * CHUNK)
-                nc.sync.dma_start(out_words[:, cols], codes[:, cols].bitcast(I32))
-        quantise(T // CHUNK - 1)
-        cols = slice(T - 2 * CHUNK, T)
-        nc.sync.dma_start(out_words[:, cols], codes[:, cols].bitcast(I32))
+        def store_codes(lo, hi):
+            nc.sync.dma_start(out_words[:, lo:hi], codes[:, lo:hi].bitcast(I32))
+
+        for t in range(2):
+            for chunk in VECTOR_CHUNKS + SCALAR_CHUNKS:
+                round_page(nc.scalar.copy, t, chunk)
+        for chunk in SCALAR_CHUNKS:
+            round_page(nc.scalar.copy, 2, chunk)
+        for chunk in SCALAR_CHUNKS:
+            round_page(nc.scalar.copy, 3, chunk)
+            weave(nc.scalar.copy, chunk)
+        va, vb = VECTOR_CHUNKS
+        s0, s1, s2, s3 = SCALAR_CHUNKS
+        vcopy = nc.vector.tensor_copy
+        round_page(vcopy, 2, va)
+        round_page(vcopy, 3, va)
+        round_page(vcopy, 2, vb)
+        weave(vcopy, va)
+        round_page(vcopy, 3, vb)
+        quantise(va)
+        store_codes(va[0], va[1])
+        weave(vcopy, vb)
+        quantise(s0)
+        quantise(s1)
+        store_codes(s0[0], s1[1])
+        quantise(vb)
+        store_codes(vb[0], vb[1])
+        quantise(s2)
+        store_codes(s2[0], s2[1])
+        quantise(s3)
+        store_codes(s3[0], s3[1])
         for q in range(4):
-            nc.scalar.dma_start(out_2[0, 4 * q : 4 * q + 4, :].bitcast(I32), code_sc[32 * q : 32 * q + 4, :].bitcast(I32))
+            queue = nc.scalar if q < 3 else nc.sync
+            queue.dma_start(out_2[0, 4 * q : 4 * q + 4, :].bitcast(I32), code_sc[32 * q : 32 * q + 4, :].bitcast(I32))

@@ -50,28 +50,29 @@ def tile_list_rgg_ownsiluP_kernel(tc, tab_words, tab_scales, wa_words, wa_scales
         tab_w = keep.tile([P, T], I32, align_bytes=64)
         nc.sync.dma_start(tab_w[:], tab_words[0].rearrange("p t i -> p (t i)").bitcast(I32))
 
-        w_sc = {}
-        for name in ("wa", "wb", "wo"):
-            w_sc[name] = keep.tile([P, PASSES, N], U8, align_bytes=64, name=name + "_sc")
-            nc.gpsimd.memset(w_sc[name][:].rearrange("p a n -> p (a n)").bitcast(I32), 0)
+        w_sc_rows = keep.tile([16, 3, PASSES, N], U8, align_bytes=64)
+        for w, scales in enumerate((wa_scales, wb_scales, wo_scales)):
+            nc.sync.dma_start(w_sc_rows[:, w].bitcast(I32), scales.rearrange("a q n -> q a n").bitcast(I32))
+        wc_raw = [keep.tile([P, 4, N], F32, name="wc_raw%d" % a) for a in range(PASSES)]
 
-        def load_scales(queue, name, scales):
-            for q in range(4):
-                queue.dma_start(w_sc[name][32 * q : 32 * q + 4].bitcast(I32),
-                                scales[:, 4 * q : 4 * q + 4, :].rearrange("a r n -> r a n").bitcast(I32))
+        def load_wc(a):
+            nc.sync.dma_start(wc_raw[a][:], wc[512 * a : 512 * (a + 1), :].rearrange("(p i) n -> p i n", i=4))
 
-        load_scales(nc.gpsimd, "wb", wb_scales)
-        load_scales(nc.gpsimd, "wo", wo_scales)
+        load_wc(0)
         wa_w = keep.tile([P, PASSES, 2 * N], U8, align_bytes=64)
         nc.sync.dma_start(wa_w[:].bitcast(I32), wa_words.rearrange("a p c -> p a c").bitcast(I32))
-        load_scales(nc.sync, "wa", wa_scales)
         wb_w = keep.tile([P, PASSES, N], I32, align_bytes=64)
         nc.sync.dma_start(wb_w[:], wb_words.rearrange("a p n i -> p a (n i)").bitcast(I32))
+        w_sc = keep.tile([P, 3, PASSES, N], U8, align_bytes=64)
+        pages = [keep.tile([P, T], F32, name="page%d" % t) for t in range(2)]
+        nc.vector.memset(pages[0][:], 0.0)
+        nc.vector.memset(w_sc[:].rearrange("p w a n -> p (w a n)").bitcast(I32), 0)
+        for q in range(4):
+            nc.sync.dma_start(w_sc[32 * q : 32 * q + 4].rearrange("p w a n -> p (w a n)").bitcast(I32),
+                              w_sc_rows[4 * q : 4 * q + 4].rearrange("p w a n -> p (w a n)").bitcast(I32))
+        load_wc(1)
         wo_w = keep.tile([P, PASSES, 2 * N], U8, align_bytes=64)
         nc.sync.dma_start(wo_w[:].bitcast(I32), wo_words.rearrange("a p c -> p a c").bitcast(I32))
-        wc_raw = [keep.tile([P, 4, N], F32, name="wc_raw%d" % a) for a in range(PASSES)]
-        for a in range(PASSES):
-            nc.sync.dma_start(wc_raw[a][:], wc[512 * a : 512 * (a + 1), :].rearrange("(p i) n -> p i n", i=4))
 
         ident = keep.tile([P, P], F32)
         make_identity(nc, ident[:])
@@ -79,12 +80,7 @@ def tile_list_rgg_ownsiluP_kernel(tc, tab_words, tab_scales, wa_words, wa_scales
         got_sc = keep.tile([P, 2, J], U8, align_bytes=64)
         got_sc1 = keep.tile([P, 2, J], U8, align_bytes=64)
         nc.vector.memset(got_sc1[:].rearrange("p l j -> p (l j)").bitcast(I32), 0)
-        pages = [keep.tile([P, T], F32, name="page%d" % t) for t in range(4)]
-        nc.vector.memset(pages[0][:, : T // 2 - 1], 0.0)
-        nc.vector.memset(pages[0][:, T // 2 - 1 :], 0.0)
-        for t in range(1, 4):
-            for c in range(0, T, 512):
-                nc.gpsimd.memset(pages[t][:, c : c + 512], 0.0)
+        nc.vector.memset(pages[1][:], 0.0)
 
         for side in (DST, SRC):
             nc.vector.tensor_copy(got_sc[:, side, :], tab_sc[:].indirect(lists[side][:]))
@@ -104,8 +100,8 @@ def tile_list_rgg_ownsiluP_kernel(tc, tab_words, tab_scales, wa_words, wa_scales
         def quantise_wc(a, half):
             cols = slice(half * N // 2, (half + 1) * N // 2)
             wc_bf = keep.tile([P, N // 2, 4], BF16, align_bytes=64, name="wc_bf", tag="stage%d" % (2 * a + half))
-            nc.scalar.copy(wc_bf[:].rearrange("p (c e) i -> p c i e", e=4),
-                           wc_raw[a][:, :, cols].rearrange("p i (c e) -> p c i e", e=4))
+            nc.scalar.copy(wc_bf[:].rearrange("p (c e) i -> p c i e", e=2),
+                           wc_raw[a][:, :, cols].rearrange("p i (c e) -> p c i e", e=2))
             nc.vector.quantize_mx(wc_w[:, a, cols].bitcast(FP8X4), wc_sc[:, a, cols], wc_bf[:].rearrange("p n i -> p (n i)"))
 
         def gather_words(piece, tag):
@@ -126,6 +122,13 @@ def tile_list_rgg_ownsiluP_kernel(tc, tab_words, tab_scales, wa_words, wa_scales
             quantise_wc(a, 1)
             gather_words(2 + a, "stage%d" % (2 * a + 1))
 
+        def late_page(tag):
+            page = keep.tile([P, T], F32, align_bytes=64, name="page%d" % len(pages), tag=tag)
+            nc.gpsimd.memset(page[:], 0.0)
+            pages.append(page)
+
+        late_page("stage3")
+
         acts = [keep.tile([P, J], F32, name="act%d" % t) for t in range(4)]
         terms = {}
 
@@ -139,6 +142,7 @@ def tile_list_rgg_ownsiluP_kernel(tc, tab_words, tab_scales, wa_words, wa_scales
             return ap.rearrange("p (m t) -> p t m", t=4)
 
         sums = {}
+        msgs = {}
 
         def gate_and_own(j, a):
             if a == 0:
@@ -147,18 +151,25 @@ def tile_list_rgg_ownsiluP_kernel(tc, tab_words, tab_scales, wa_words, wa_scales
                 sums[j] = (za, ow)
             za, ow = sums[j]
             last = a == PASSES - 1
-            product(za, j, DST, a, wa_w[:, a, :].bitcast(FP4X4), w_sc["wa"][:, a, :], a == 0, False)
-            product(za, j, SRC, a, wb_w[:, a, :].bitcast(FP8X4), w_sc["wb"][:, a, :], False, last)
-            product(ow, j, DST, a, wo_w[:, a, :].bitcast(FP4X4), w_sc["wo"][:, a, :], a == 0, last)
+            product(za, j, DST, a, wa_w[:, a, :].bitcast(FP4X4), w_sc[:, 0, a, :], a == 0, False)
+            product(za, j, SRC, a, wb_w[:, a, :].bitcast(FP8X4), w_sc[:, 1, a, :], False, last)
+            product(ow, j, DST, a, wo_w[:, a, :].bitcast(FP4X4), w_sc[:, 2, a, :], a == 0, last)
 
-        def message(j):
+        def message(j, a):
+            if a == 0:
+                ms = psum.tile([P, N], F32)
+                msgs[j] = ms
+            product(msgs[j], j, SRC, a, wc_w[:, a, :].bitcast(FP8X4), wc_sc[:, a, :], a == 0, a == PASSES - 1)
+
+        def combine(j):
             za, ow = sums[j]
-            ms = psum.tile([P, N], F32)
-            for a in range(PASSES):
-                product(ms, j, SRC, a, wc_w[:, a, :].bitcast(FP8X4), wc_sc[:, a, :], a == 0, a == PASSES - 1)
+            ms = msgs[j]
             th = ring.tile([P, 4, P], F32)
             nc.scalar.activation(th[:], dealt(za[:]), ACT.Tanh, scale=0.5)
-            own2 = ring.tile([P, 4, P], F32)
+            if j == 0:
+                own2 = keep.tile([P, 4, P], F32, align_bytes=64, tag="own_page")
+            else:
+                own2 = ring.tile([P, 4, P], F32)
             nc.scalar.activation(own2[:], dealt(ow[:]), ACT.Copy, scale=2.0)
             msg2 = ring.tile([P, 4, P], F32)
             nc.vector.scalar_tensor_tensor(msg2[:], th[:], 1.0, dealt(ms[:]), ALU.add, ALU.mult)
@@ -167,7 +178,9 @@ def tile_list_rgg_ownsiluP_kernel(tc, tab_words, tab_scales, wa_words, wa_scales
         def multiply(j):
             for a in range(PASSES):
                 gate_and_own(j, a)
-            message(j)
+            for a in range(PASSES):
+                message(j, a)
+            combine(j)
 
         def turn(j):
             own2, msg2 = terms[j]
@@ -187,9 +200,12 @@ def tile_list_rgg_ownsiluP_kernel(tc, tab_words, tab_scales, wa_words, wa_scales
         for a in range(PASSES):
             gate_and_own(0, a)
             gate_and_own(1, a)
-        message(0)
-        message(1)
+            message(0, a)
+            message(1, a)
+        combine(0)
+        combine(1)
         turn(0)
+        late_page("own_page")
         for j in range(2, 5):
             multiply(j)
             if j < 4:
@@ -219,7 +235,7 @@ def tile_list_rgg_ownsiluP_kernel(tc, tab_words, tab_scales, wa_words, wa_scales
 
         def weave(copy, chunk):
             words = pairs[chunk][:].rearrange("p h c e -> p h (c e)").bitcast(F32)
-            copy(woven[chunk][:].bitcast(F32), words.rearrange("p h c -> p c h"))
+            copy(woven[chunk][:].bitcast(F32).rearrange("p (c e) h -> p c h e", e=2), words.rearrange("p h (c e) -> p c h e", e=2))
 
         def quantise(chunk):
             cols = slice(chunk[0], chunk[1])

@@ -24,12 +24,6 @@ PIECE = 256
 VECTOR_CHUNKS = ((0, 512), (512, 1024))
 SCALAR_CHUNKS = ((1024, 1280), (1280, 1536), (1536, 1792), (1792, 2048))
 SRC, DST = 0, 1
-SCATTER_RUNS = (
-    ((0, 2), (2, 4), (4, 6), (6, 8)),
-    ((0, 2), (2, 4), (4, 6), (6, 8)),
-    ((0, 3), (3, 5), (5, 8)),
-    ((0, 3), (3, 8)),
-)
 
 
 def tile_list_rgg_ownsiluP_kernel(tc, tab_words, tab_scales, wa_words, wa_scales, wb_words, wb_scales, wc,
@@ -37,61 +31,64 @@ def tile_list_rgg_ownsiluP_kernel(tc, tab_words, tab_scales, wa_words, wa_scales
     nc = tc.nc
     with ExitStack() as ctx:
         keep = ctx.enter_context(tc.tile_pool(name="keep", bufs=1))
-        ring = ctx.enter_context(tc.tile_pool(name="ring", bufs=3))
         psum = ctx.enter_context(tc.psum_pool(name="psum", bufs=2))
 
         lists = [keep.tile([P, J // 16], U16, name="list_src"), keep.tile([P, J // 16], U16, name="list_dst")]
-        tab_sc = keep.tile([P, T], U8, align_bytes=64, tag="early_late")
-        nc.gpsimd.memset(tab_sc[:].bitcast(I32), 0)
         nc.sync.dma_start(lists[DST][:], offs2)
         nc.sync.dma_start(lists[SRC][:], offs)
-        for q in range(4):
-            nc.sync.dma_start(tab_sc[32 * q : 32 * q + 8, :].bitcast(I32), tab_scales[:, 4 * q : 4 * q + 4, :].bitcast(I32))
-        tab_w = keep.tile([P, T], I32, align_bytes=64)
-        nc.sync.dma_start(tab_w[:], tab_words[0].rearrange("p t i -> p (t i)").bitcast(I32))
-
-        w_sc_rows = keep.tile([16, 3, PASSES, N], U8, align_bytes=64)
+        tab_sc = keep.tile([P, T], U8, align_bytes=64, tag="early_late")
+        nc.sync.dma_start(tab_sc[0:32, :].bitcast(I32), tab_scales.rearrange("a q t -> q a t").bitcast(I32))
+        nc.vector.memset(tab_sc[32:64, :].bitcast(I32), 0)
+        nc.vector.memset(tab_sc[64:128, :].bitcast(I32), 0)
+        w_sc_rows = keep.tile([16, 3, PASSES, N], U8, align_bytes=64, tag="rows_bias")
         for w, scales in enumerate((wa_scales, wb_scales, wo_scales)):
             nc.sync.dma_start(w_sc_rows[:, w].bitcast(I32), scales.rearrange("a q n -> q a n").bitcast(I32))
-        wc_raw = [keep.tile([P, 4, N], F32, name="wc_raw%d" % a) for a in range(PASSES)]
-
-        def load_wc(a):
-            nc.sync.dma_start(wc_raw[a][:], wc[512 * a : 512 * (a + 1), :].rearrange("(p i) n -> p i n", i=4))
-
-        load_wc(0)
+        tab_w = keep.tile([P, T], I32, align_bytes=64)
+        nc.sync.dma_start(tab_w[:], tab_words[0].rearrange("p t i -> p (t i)").bitcast(I32))
+        wc_rows = wc.rearrange("(a p i) n -> a p i n", a=PASSES, i=4)
+        wc_raw = {}
+        wc_first = keep.tile([P, 4, N], F32)
+        nc.sync.dma_start(wc_first[:], wc_rows[0])
+        for half in range(2):
+            wc_raw[0, half] = wc_first[:, :, half * N // 2 : (half + 1) * N // 2]
+        w_sc = keep.tile([P, 3, PASSES, N], U8, align_bytes=64)
+        nc.vector.memset(w_sc[:].rearrange("p w a n -> p (w a n)").bitcast(I32), 0)
+        node_sc = keep.tile([P, PASSES, 2, J], U8, align_bytes=64)
+        nc.vector.memset(node_sc[:].rearrange("p a l j -> p (a l j)").bitcast(I32), 0)
+        for q in range(4):
+            nc.sync.dma_start(w_sc[32 * q : 32 * q + 4].rearrange("p w a n -> p (w a n)").bitcast(I32),
+                              w_sc_rows[4 * q : 4 * q + 4].rearrange("p w a n -> p (w a n)").bitcast(I32))
         wa_w = keep.tile([P, PASSES, 2 * N], U8, align_bytes=64)
         nc.sync.dma_start(wa_w[:].bitcast(I32), wa_words.rearrange("a p c -> p a c").bitcast(I32))
         wb_w = keep.tile([P, PASSES, N], I32, align_bytes=64)
         nc.sync.dma_start(wb_w[:], wb_words.rearrange("a p n i -> p a (n i)").bitcast(I32))
-        w_sc = keep.tile([P, 3, PASSES, N], U8, align_bytes=64)
-        pages = [keep.tile([P, T], F32, name="page%d" % t) for t in range(2)]
-        nc.vector.memset(pages[0][:], 0.0)
-        nc.vector.memset(w_sc[:].rearrange("p w a n -> p (w a n)").bitcast(I32), 0)
-        for q in range(4):
-            nc.sync.dma_start(w_sc[32 * q : 32 * q + 4].rearrange("p w a n -> p (w a n)").bitcast(I32),
-                              w_sc_rows[4 * q : 4 * q + 4].rearrange("p w a n -> p (w a n)").bitcast(I32))
-        load_wc(1)
         wo_w = keep.tile([P, PASSES, 2 * N], U8, align_bytes=64)
         nc.sync.dma_start(wo_w[:].bitcast(I32), wo_words.rearrange("a p c -> p a c").bitcast(I32))
 
         ident = keep.tile([P, P], F32)
         make_identity(nc, ident[:])
 
-        got_sc = keep.tile([P, 2, J], U8, align_bytes=64)
-        got_sc1 = keep.tile([P, 2, J], U8, align_bytes=64)
-        nc.vector.memset(got_sc1[:].rearrange("p l j -> p (l j)").bitcast(I32), 0)
-        nc.vector.memset(pages[1][:], 0.0)
-
+        got_sc = keep.tile([P, 2, J], U8, align_bytes=64, tag="got_gate")
         for side in (DST, SRC):
             nc.vector.tensor_copy(got_sc[:, side, :], tab_sc[:].indirect(lists[side][:]))
         for q in range(4):
-            nc.sync.dma_start(got_sc1[32 * q : 32 * q + 4].rearrange("p l j -> p (l j)").bitcast(I32),
-                                got_sc[32 * q + 4 : 32 * q + 8].rearrange("p l j -> p (l j)").bitcast(I32))
-        bias = keep.tile([P, 4], F32)
+            nc.sync.dma_start(node_sc[32 * q : 32 * q + 4].rearrange("p a l j -> p a (l j)").bitcast(I32),
+                              got_sc[8 * q : 8 * q + 8].rearrange("p l j -> p (l j)").bitcast(I32))
+        for half in range(2):
+            wc_second = keep.tile([P, 4, N // 2], F32, name="wc_second%d" % half)
+            nc.sync.dma_start(wc_second[:], wc_rows[1][:, :, half * N // 2 : (half + 1) * N // 2])
+            wc_raw[1, half] = wc_second[:]
+        bias = keep.tile([P, 4], F32, align_bytes=64, tag="rows_bias")
         nc.sync.dma_start(bias[:], b.rearrange("(p t) -> p t", t=4))
-        gate_w = keep.tile([P, J], F32, align_bytes=64, tag="early_late")
+        gate_w = keep.tile([P, J], F32, align_bytes=64, tag="got_gate")
         nc.sync.dma_start(gate_w[:], wgo)
-        node_sc = (got_sc, got_sc1)
+
+        pages = {}
+
+        def clear_page(t, tag):
+            page = keep.tile([P, T], F32, align_bytes=64, name="page%d" % t, tag=tag)
+            nc.vector.memset(page[:], 0.0)
+            pages[t] = page
 
         wc_w = keep.tile([P, PASSES, N], U32, align_bytes=64)
         wc_sc = keep.tile([P, PASSES, N], U8, align_bytes=64)
@@ -101,7 +98,7 @@ def tile_list_rgg_ownsiluP_kernel(tc, tab_words, tab_scales, wa_words, wa_scales
             cols = slice(half * N // 2, (half + 1) * N // 2)
             wc_bf = keep.tile([P, N // 2, 4], BF16, align_bytes=64, name="wc_bf", tag="stage%d" % (2 * a + half))
             nc.scalar.copy(wc_bf[:].rearrange("p (c e) i -> p c i e", e=2),
-                           wc_raw[a][:, :, cols].rearrange("p i (c e) -> p c i e", e=2))
+                           wc_raw[a, half].rearrange("p i (c e) -> p c i e", e=2))
             nc.vector.quantize_mx(wc_w[:, a, cols].bitcast(FP8X4), wc_sc[:, a, cols], wc_bf[:].rearrange("p n i -> p (n i)"))
 
         def gather_words(piece, tag):
@@ -116,105 +113,84 @@ def tile_list_rgg_ownsiluP_kernel(tc, tab_words, tab_scales, wa_words, wa_scales
                 node_w[j] = (parted, j * P - first)
 
         gather_words(0, "got0")
-        gather_words(1, "got1")
         for a in range(PASSES):
             quantise_wc(a, 0)
             quantise_wc(a, 1)
-            gather_words(2 + a, "stage%d" % (2 * a + 1))
+        for t, tag in enumerate(("got0", "stage0", "stage1")):
+            clear_page(t, tag)
+        gather_words(1, "stage3")
 
-        def late_page(tag):
-            page = keep.tile([P, T], F32, align_bytes=64, name="page%d" % len(pages), tag=tag)
-            nc.gpsimd.memset(page[:], 0.0)
-            pages.append(page)
-
-        late_page("stage3")
-
-        acts = [keep.tile([P, J], F32, name="act%d" % t) for t in range(4)]
         terms = {}
 
         def product(acc, j, side, a, w, w_scale, start, stop):
             parted, col = node_w[j]
             nc.tensor.matmul_mx(acc[:], lhsT=parted[:, side, a, 2 * col : 2 * col + 2 * P].bitcast(FP4X4),
-                                lhsT_scale=node_sc[a][:, side, j * P : (j + 1) * P],
+                                lhsT_scale=node_sc[:, a, side, j * P : (j + 1) * P],
                                 rhs=w, rhs_scale=w_scale, start=start, stop=stop)
 
         def dealt(ap):
             return ap.rearrange("p (m t) -> p t m", t=4)
 
-        sums = {}
-        msgs = {}
-
-        def gate_and_own(j, a):
-            if a == 0:
-                za = psum.tile([P, N], F32)
-                ow = psum.tile([P, N], F32)
-                sums[j] = (za, ow)
-            za, ow = sums[j]
-            last = a == PASSES - 1
-            product(za, j, DST, a, wa_w[:, a, :].bitcast(FP4X4), w_sc[:, 0, a, :], a == 0, False)
-            product(za, j, SRC, a, wb_w[:, a, :].bitcast(FP8X4), w_sc[:, 1, a, :], False, last)
-            product(ow, j, DST, a, wo_w[:, a, :].bitcast(FP4X4), w_sc[:, 2, a, :], a == 0, last)
-
-        def message(j, a):
-            if a == 0:
-                ms = psum.tile([P, N], F32)
-                msgs[j] = ms
-            product(msgs[j], j, SRC, a, wc_w[:, a, :].bitcast(FP8X4), wc_sc[:, a, :], a == 0, a == PASSES - 1)
-
-        def combine(j):
-            za, ow = sums[j]
-            ms = msgs[j]
-            th = ring.tile([P, 4, P], F32)
+        def multiply(j):
+            za = psum.tile([P, N], F32)
+            ow = psum.tile([P, N], F32)
+            ms = psum.tile([P, N], F32)
+            for a in range(PASSES):
+                product(za, j, DST, a, wa_w[:, a, :].bitcast(FP4X4), w_sc[:, 0, a, :], a == 0, False)
+                product(za, j, SRC, a, wb_w[:, a, :].bitcast(FP8X4), w_sc[:, 1, a, :], False, a == PASSES - 1)
+            for a in range(PASSES):
+                product(ow, j, DST, a, wo_w[:, a, :].bitcast(FP4X4), w_sc[:, 2, a, :], a == 0, a == PASSES - 1)
+            for a in range(PASSES):
+                product(ms, j, SRC, a, wc_w[:, a, :].bitcast(FP8X4), wc_sc[:, a, :], a == 0, a == PASSES - 1)
+            th = keep.tile([P, 4, P], F32, align_bytes=64, name="th", tag="th%d" % j)
             nc.scalar.activation(th[:], dealt(za[:]), ACT.Tanh, scale=0.5)
-            if j == 0:
-                own2 = keep.tile([P, 4, P], F32, align_bytes=64, tag="own_page")
-            else:
-                own2 = ring.tile([P, 4, P], F32)
+            own2 = keep.tile([P, 4, P], F32, name="own%d" % j)
             nc.scalar.activation(own2[:], dealt(ow[:]), ACT.Copy, scale=2.0)
-            msg2 = ring.tile([P, 4, P], F32)
+            msg2 = keep.tile([P, 4, P], F32, name="msg%d" % j)
             nc.vector.scalar_tensor_tensor(msg2[:], th[:], 1.0, dealt(ms[:]), ALU.add, ALU.mult)
             terms[j] = (own2, msg2)
 
-        def multiply(j):
-            for a in range(PASSES):
-                gate_and_own(j, a)
-            for a in range(PASSES):
-                message(j, a)
-            combine(j)
+        acts = [keep.tile([P, J], F32, name="act%d" % t) for t in range(4)]
 
-        def turn(j):
-            own2, msg2 = terms[j]
+        def turn(t, lo, hi):
             turned = psum.tile([P, 4, P], F32)
-            for t in range(4):
-                nc.tensor.matmul(turned[:, t, :], lhsT=own2[:, t, :], rhs=ident[:], start=True, stop=False, is_transpose=True)
-                nc.tensor.matmul(turned[:, t, :], lhsT=msg2[:, t, :], rhs=ident[:], start=False, stop=True, is_transpose=True)
-            for t in range(4):
-                nc.scalar.activation(acts[t][:, j * P : (j + 1) * P], turned[:, t, :], ACT.Silu, bias=bias[:, t : t + 1], scale=0.5)
-            for t in range(4):
-                for lo, hi in SCATTER_RUNS[t]:
-                    if hi == j + 1:
-                        cols = slice(lo * P, hi * P)
-                        nc.vector.tensor_tensor(pages[t][:].indirect(lists[DST][:, lo * 8 : hi * 8]),
-                                                acts[t][:, cols], gate_w[:, cols], ALU.mult)
+            for j in range(lo, hi):
+                own2, msg2 = terms[j]
+                nc.tensor.matmul(turned[:, j - lo, :], lhsT=own2[:, t, :], rhs=ident[:], start=True, stop=False, is_transpose=True)
+                nc.tensor.matmul(turned[:, j - lo, :], lhsT=msg2[:, t, :], rhs=ident[:], start=False, stop=True, is_transpose=True)
+            nc.scalar.activation(acts[t][:, lo * P : hi * P], turned[:, 0 : hi - lo, :].rearrange("p j m -> p (j m)"),
+                                 ACT.Silu, bias=bias[:, t : t + 1], scale=0.5)
 
-        for a in range(PASSES):
-            gate_and_own(0, a)
-            gate_and_own(1, a)
-            message(0, a)
-            message(1, a)
-        combine(0)
-        combine(1)
-        turn(0)
-        late_page("own_page")
-        for j in range(2, 5):
+        def place(t, lo, hi):
+            cols = slice(lo * P, hi * P)
+            nc.vector.tensor_tensor(pages[t][:].indirect(lists[DST][:, lo * 8 : hi * 8]), acts[t][:, cols], gate_w[:, cols], ALU.mult)
+
+        def job(t, lo, hi):
+            turn(t, lo, hi)
+            place(t, lo, hi)
+
+        multiply(0)
+        multiply(1)
+        gather_words(2, "th1")
+        gather_words(3, "th1")
+        multiply(2)
+        job(0, 0, 2)
+        job(1, 0, 2)
+        multiply(3)
+        job(2, 0, 2)
+        for j in range(4, EDGE_TILES):
             multiply(j)
-            if j < 4:
-                turn(j - 1)
-        for j in range(5, EDGE_TILES):
-            multiply(j)
-            turn(j - 2)
-        turn(EDGE_TILES - 2)
-        turn(EDGE_TILES - 1)
+            if j == 5:
+                clear_page(3, "th5")
+            job(j % 2, j // 2 * 2 - 2, j // 2 * 2)
+        job(0, 6, 8)
+        job(1, 6, 8)
+        turn(2, 2, 5)
+        turn(2, 5, 8)
+        place(2, 2, 8)
+        turn(3, 0, 4)
+        turn(3, 4, 8)
+        place(3, 0, 8)
 
         out_rows = out_0.rearrange("(p t) c -> p t c", t=4)
         for t in range(4):

@@ -85,9 +85,9 @@ def tile_list_rgg_ownsiluP_kernel(tc, tab_words, tab_scales, wa_words, wa_scales
 
         pages = {}
 
-        def clear_page(t, tag):
+        def clear_page(t, tag, engine):
             page = keep.tile([P, T], F32, align_bytes=64, name="page%d" % t, tag=tag)
-            nc.vector.memset(page[:], 0.0)
+            engine.memset(page[:], 0.0)
             pages[t] = page
 
         wc_w = keep.tile([P, PASSES, N], U32, align_bytes=64)
@@ -116,8 +116,8 @@ def tile_list_rgg_ownsiluP_kernel(tc, tab_words, tab_scales, wa_words, wa_scales
         for a in range(PASSES):
             quantise_wc(a, 0)
             quantise_wc(a, 1)
-        for t, tag in enumerate(("got0", "stage0", "stage1")):
-            clear_page(t, tag)
+        for t, tag in enumerate(("got0", "stage0")):
+            clear_page(t, tag, nc.vector)
         gather_words(1, "stage3")
 
         terms = {}
@@ -174,23 +174,26 @@ def tile_list_rgg_ownsiluP_kernel(tc, tab_words, tab_scales, wa_words, wa_scales
         gather_words(2, "th1")
         gather_words(3, "th1")
         multiply(2)
+        clear_page(2, "th2", nc.gpsimd)
         job(0, 0, 2)
         job(1, 0, 2)
         multiply(3)
+        clear_page(3, "th3", nc.gpsimd)
         job(2, 0, 2)
-        for j in range(4, EDGE_TILES):
-            multiply(j)
-            if j == 5:
-                clear_page(3, "th5")
-            job(j % 2, j // 2 * 2 - 2, j // 2 * 2)
+        multiply(4)
+        job(0, 2, 4)
+        job(1, 2, 4)
+        multiply(5)
+        job(2, 2, 4)
+        job(3, 0, 4)
+        multiply(6)
+        job(0, 4, 6)
+        multiply(7)
+        job(1, 4, 6)
         job(0, 6, 8)
         job(1, 6, 8)
-        turn(2, 2, 5)
-        turn(2, 5, 8)
-        place(2, 2, 8)
-        turn(3, 0, 4)
-        turn(3, 4, 8)
-        place(3, 0, 8)
+        job(2, 4, 8)
+        job(3, 4, 8)
 
         out_rows = out_0.rearrange("(p t) c -> p t c", t=4)
         for t in range(4):

@@ -34,54 +34,57 @@ def tile_list_rgg_ownsiluP_kernel(tc, tab_words, tab_scales, wa_words, wa_scales
         psum = ctx.enter_context(tc.psum_pool(name="psum", bufs=2))
 
         lists = [keep.tile([P, J // 16], U16, name="list_src"), keep.tile([P, J // 16], U16, name="list_dst")]
+        tab_sc = keep.tile([P, T], U8, align_bytes=64, tag="early_late")
+        nc.gpsimd.memset(tab_sc[:].bitcast(I32), 0)
         nc.sync.dma_start(lists[DST][:], offs2)
         nc.sync.dma_start(lists[SRC][:], offs)
-        tab_sc = keep.tile([P, T], U8, align_bytes=64, tag="early_late")
-        nc.sync.dma_start(tab_sc[0:32, :].bitcast(I32), tab_scales.rearrange("a q t -> q a t").bitcast(I32))
-        nc.vector.memset(tab_sc[32:64, :].bitcast(I32), 0)
-        nc.vector.memset(tab_sc[64:128, :].bitcast(I32), 0)
-        w_sc_rows = keep.tile([16, 3, PASSES, N], U8, align_bytes=64, tag="rows_bias")
-        for w, scales in enumerate((wa_scales, wb_scales, wo_scales)):
-            nc.sync.dma_start(w_sc_rows[:, w].bitcast(I32), scales.rearrange("a q n -> q a n").bitcast(I32))
+        for q in range(4):
+            nc.sync.dma_start(tab_sc[32 * q : 32 * q + 8, :].bitcast(I32), tab_scales[:, 4 * q : 4 * q + 4, :].bitcast(I32))
         tab_w = keep.tile([P, T], I32, align_bytes=64)
         nc.sync.dma_start(tab_w[:], tab_words[0].rearrange("p t i -> p (t i)").bitcast(I32))
+
+        w_sc_rows = keep.tile([16, 3, PASSES, N], U8, align_bytes=64)
+        for w, scales in enumerate((wa_scales, wb_scales, wo_scales)):
+            nc.sync.dma_start(w_sc_rows[:, w].bitcast(I32), scales.rearrange("a q n -> q a n").bitcast(I32))
         wc_rows = wc.rearrange("(a p i) n -> a p i n", a=PASSES, i=4)
         wc_raw = {}
-        wc_first = keep.tile([P, 4, N], F32)
-        nc.sync.dma_start(wc_first[:], wc_rows[0])
-        for half in range(2):
-            wc_raw[0, half] = wc_first[:, :, half * N // 2 : (half + 1) * N // 2]
-        w_sc = keep.tile([P, 3, PASSES, N], U8, align_bytes=64)
-        nc.vector.memset(w_sc[:].rearrange("p w a n -> p (w a n)").bitcast(I32), 0)
-        node_sc = keep.tile([P, PASSES, 2, J], U8, align_bytes=64)
-        nc.vector.memset(node_sc[:].rearrange("p a l j -> p (a l j)").bitcast(I32), 0)
-        for q in range(4):
-            nc.sync.dma_start(w_sc[32 * q : 32 * q + 4].rearrange("p w a n -> p (w a n)").bitcast(I32),
-                              w_sc_rows[4 * q : 4 * q + 4].rearrange("p w a n -> p (w a n)").bitcast(I32))
+
+        def load_wc(a):
+            wc_pass = keep.tile([P, 4, N], F32, name="wc_pass%d" % a)
+            nc.sync.dma_start(wc_pass[:], wc_rows[a])
+            for half in range(2):
+                wc_raw[a, half] = wc_pass[:, :, half * N // 2 : (half + 1) * N // 2]
+
+        load_wc(0)
         wa_w = keep.tile([P, PASSES, 2 * N], U8, align_bytes=64)
         nc.sync.dma_start(wa_w[:].bitcast(I32), wa_words.rearrange("a p c -> p a c").bitcast(I32))
         wb_w = keep.tile([P, PASSES, N], I32, align_bytes=64)
         nc.sync.dma_start(wb_w[:], wb_words.rearrange("a p n i -> p a (n i)").bitcast(I32))
+        w_sc = keep.tile([P, 3, PASSES, N], U8, align_bytes=64)
+        nc.vector.memset(w_sc[:].rearrange("p w a n -> p (w a n)").bitcast(I32), 0)
+        for q in range(4):
+            nc.sync.dma_start(w_sc[32 * q : 32 * q + 4].rearrange("p w a n -> p (w a n)").bitcast(I32),
+                              w_sc_rows[4 * q : 4 * q + 4].rearrange("p w a n -> p (w a n)").bitcast(I32))
+        load_wc(1)
         wo_w = keep.tile([P, PASSES, 2 * N], U8, align_bytes=64)
         nc.sync.dma_start(wo_w[:].bitcast(I32), wo_words.rearrange("a p c -> p a c").bitcast(I32))
 
         ident = keep.tile([P, P], F32)
         make_identity(nc, ident[:])
 
-        got_sc = keep.tile([P, 2, J], U8, align_bytes=64, tag="got_gate")
+        got_sc = keep.tile([P, 2, J], U8, align_bytes=64)
+        got_sc1 = keep.tile([P, 2, J], U8, align_bytes=64)
+        nc.vector.memset(got_sc1[:].rearrange("p l j -> p (l j)").bitcast(I32), 0)
         for side in (DST, SRC):
             nc.vector.tensor_copy(got_sc[:, side, :], tab_sc[:].indirect(lists[side][:]))
         for q in range(4):
-            nc.sync.dma_start(node_sc[32 * q : 32 * q + 4].rearrange("p a l j -> p a (l j)").bitcast(I32),
-                              got_sc[8 * q : 8 * q + 8].rearrange("p l j -> p (l j)").bitcast(I32))
-        for half in range(2):
-            wc_second = keep.tile([P, 4, N // 2], F32, name="wc_second%d" % half)
-            nc.sync.dma_start(wc_second[:], wc_rows[1][:, :, half * N // 2 : (half + 1) * N // 2])
-            wc_raw[1, half] = wc_second[:]
-        bias = keep.tile([P, 4], F32, align_bytes=64, tag="rows_bias")
+            nc.sync.dma_start(got_sc1[32 * q : 32 * q + 4].rearrange("p l j -> p (l j)").bitcast(I32),
+                              got_sc[32 * q + 4 : 32 * q + 8].rearrange("p l j -> p (l j)").bitcast(I32))
+        bias = keep.tile([P, 4], F32)
         nc.sync.dma_start(bias[:], b.rearrange("(p t) -> p t", t=4))
-        gate_w = keep.tile([P, J], F32, align_bytes=64, tag="got_gate")
+        gate_w = keep.tile([P, J], F32, align_bytes=64, tag="early_late")
         nc.sync.dma_start(gate_w[:], wgo)
+        node_sc = (got_sc, got_sc1)
 
         pages = {}
 
@@ -112,36 +115,47 @@ def tile_list_rgg_ownsiluP_kernel(tc, tab_words, tab_scales, wa_words, wa_scales
             for j in range(first // P, (first + PIECE) // P):
                 node_w[j] = (parted, j * P - first)
 
+        clear_page(0, "page0", nc.vector)
         gather_words(0, "got0")
+        gather_words(1, "got1")
         for a in range(PASSES):
             quantise_wc(a, 0)
             quantise_wc(a, 1)
-        for t, tag in enumerate(("got0", "stage0")):
-            clear_page(t, tag, nc.vector)
-        gather_words(1, "stage3")
+        gather_words(2, "stage1")
 
         terms = {}
 
         def product(acc, j, side, a, w, w_scale, start, stop):
             parted, col = node_w[j]
             nc.tensor.matmul_mx(acc[:], lhsT=parted[:, side, a, 2 * col : 2 * col + 2 * P].bitcast(FP4X4),
-                                lhsT_scale=node_sc[:, a, side, j * P : (j + 1) * P],
+                                lhsT_scale=node_sc[a][:, side, j * P : (j + 1) * P],
                                 rhs=w, rhs_scale=w_scale, start=start, stop=stop)
 
         def dealt(ap):
             return ap.rearrange("p (m t) -> p t m", t=4)
 
+        sums = {}
+
+        def run_pass(j, a):
+            if a == 0:
+                za = psum.tile([P, N], F32)
+                ow = psum.tile([P, N], F32)
+                ms = psum.tile([P, N], F32)
+                sums[j] = (za, ow, ms)
+            za, ow, ms = sums[j]
+            last = a == PASSES - 1
+            product(za, j, DST, a, wa_w[:, a, :].bitcast(FP4X4), w_sc[:, 0, a, :], a == 0, False)
+            product(za, j, SRC, a, wb_w[:, a, :].bitcast(FP8X4), w_sc[:, 1, a, :], False, last)
+            product(ow, j, DST, a, wo_w[:, a, :].bitcast(FP4X4), w_sc[:, 2, a, :], a == 0, last)
+            product(ms, j, SRC, a, wc_w[:, a, :].bitcast(FP8X4), wc_sc[:, a, :], a == 0, last)
+
         def multiply(j):
-            za = psum.tile([P, N], F32)
-            ow = psum.tile([P, N], F32)
-            ms = psum.tile([P, N], F32)
             for a in range(PASSES):
-                product(za, j, DST, a, wa_w[:, a, :].bitcast(FP4X4), w_sc[:, 0, a, :], a == 0, False)
-                product(za, j, SRC, a, wb_w[:, a, :].bitcast(FP8X4), w_sc[:, 1, a, :], False, a == PASSES - 1)
-            for a in range(PASSES):
-                product(ow, j, DST, a, wo_w[:, a, :].bitcast(FP4X4), w_sc[:, 2, a, :], a == 0, a == PASSES - 1)
-            for a in range(PASSES):
-                product(ms, j, SRC, a, wc_w[:, a, :].bitcast(FP8X4), wc_sc[:, a, :], a == 0, a == PASSES - 1)
+                run_pass(j, a)
+            combine(j)
+
+        def combine(j):
+            za, ow, ms = sums[j]
             th = keep.tile([P, 4, P], F32, align_bytes=64, name="th", tag="th%d" % j)
             nc.scalar.activation(th[:], dealt(za[:]), ACT.Tanh, scale=0.5)
             own2 = keep.tile([P, 4, P], F32, name="own%d" % j)
@@ -169,14 +183,17 @@ def tile_list_rgg_ownsiluP_kernel(tc, tab_words, tab_scales, wa_words, wa_scales
             turn(t, lo, hi)
             place(t, lo, hi)
 
-        multiply(0)
-        multiply(1)
-        gather_words(2, "th1")
+        for a in range(PASSES):
+            run_pass(0, a)
+            run_pass(1, a)
+        combine(0)
+        combine(1)
         gather_words(3, "th1")
-        multiply(2)
-        clear_page(2, "th2", nc.gpsimd)
+        clear_page(1, "th1", nc.gpsimd)
         job(0, 0, 2)
         job(1, 0, 2)
+        multiply(2)
+        clear_page(2, "th2", nc.gpsimd)
         multiply(3)
         clear_page(3, "th3", nc.gpsimd)
         job(2, 0, 2)

@@ -42,10 +42,6 @@ def tile_list_rgg_ownsiluP_kernel(tc, tab_words, tab_scales, wa_words, wa_scales
             nc.sync.dma_start(tab_sc[32 * q : 32 * q + 8, :].bitcast(I32), tab_scales[:, 4 * q : 4 * q + 4, :].bitcast(I32))
         tab_w = keep.tile([P, T], I32, align_bytes=64)
         nc.sync.dma_start(tab_w[:], tab_words[0].rearrange("p t i -> p (t i)").bitcast(I32))
-
-        w_sc_rows = keep.tile([16, 3, PASSES, N], U8, align_bytes=64)
-        for w, scales in enumerate((wa_scales, wb_scales, wo_scales)):
-            nc.sync.dma_start(w_sc_rows[:, w].bitcast(I32), scales.rearrange("a q n -> q a n").bitcast(I32))
         wc_rows = wc.rearrange("(a p i) n -> a p i n", a=PASSES, i=4)
         wc_raw = {}
 
@@ -56,18 +52,19 @@ def tile_list_rgg_ownsiluP_kernel(tc, tab_words, tab_scales, wa_words, wa_scales
                 wc_raw[a, half] = wc_pass[:, :, half * N // 2 : (half + 1) * N // 2]
 
         load_wc(0)
+        w_sc_rows = keep.tile([16, 3, PASSES, N], U8, align_bytes=64)
+        for w, scales in enumerate((wa_scales, wb_scales, wo_scales)):
+            nc.sync.dma_start(w_sc_rows[:, w].bitcast(I32), scales.rearrange("a q n -> q a n").bitcast(I32))
+        load_wc(1)
+        w_sc = keep.tile([P, 3, PASSES, N], U8, align_bytes=64)
+        nc.vector.memset(w_sc[:].rearrange("p w a n -> p (w a n)").bitcast(I32), 0)
+        for r in range(4):
+            nc.sync.dma_start(w_sc[r:P:32].rearrange("p w a n -> p (w a n)").bitcast(I32),
+                              w_sc_rows[r:16:4].rearrange("p w a n -> p (w a n)").bitcast(I32))
         wa_w = keep.tile([P, PASSES, 2 * N], U8, align_bytes=64)
         nc.sync.dma_start(wa_w[:].bitcast(I32), wa_words.rearrange("a p c -> p a c").bitcast(I32))
         wb_w = keep.tile([P, PASSES, N], I32, align_bytes=64)
         nc.sync.dma_start(wb_w[:], wb_words.rearrange("a p n i -> p a (n i)").bitcast(I32))
-        w_sc = keep.tile([P, 3, PASSES, N], U8, align_bytes=64)
-        nc.vector.memset(w_sc[:].rearrange("p w a n -> p (w a n)").bitcast(I32), 0)
-        for q in range(4):
-            nc.sync.dma_start(w_sc[32 * q : 32 * q + 4].rearrange("p w a n -> p (w a n)").bitcast(I32),
-                              w_sc_rows[4 * q : 4 * q + 4].rearrange("p w a n -> p (w a n)").bitcast(I32))
-        load_wc(1)
-        wo_w = keep.tile([P, PASSES, 2 * N], U8, align_bytes=64)
-        nc.sync.dma_start(wo_w[:].bitcast(I32), wo_words.rearrange("a p c -> p a c").bitcast(I32))
 
         ident = keep.tile([P, P], F32)
         make_identity(nc, ident[:])
@@ -77,13 +74,15 @@ def tile_list_rgg_ownsiluP_kernel(tc, tab_words, tab_scales, wa_words, wa_scales
         nc.vector.memset(got_sc1[:].rearrange("p l j -> p (l j)").bitcast(I32), 0)
         for side in (DST, SRC):
             nc.vector.tensor_copy(got_sc[:, side, :], tab_sc[:].indirect(lists[side][:]))
-        for q in range(4):
-            nc.sync.dma_start(got_sc1[32 * q : 32 * q + 4].rearrange("p l j -> p (l j)").bitcast(I32),
-                              got_sc[32 * q + 4 : 32 * q + 8].rearrange("p l j -> p (l j)").bitcast(I32))
-        bias = keep.tile([P, 4], F32)
-        nc.sync.dma_start(bias[:], b.rearrange("(p t) -> p t", t=4))
+        for r in range(4):
+            nc.sync.dma_start(got_sc1[r:P:32].rearrange("p l j -> p (l j)").bitcast(I32),
+                              got_sc[4 + r : P : 32].rearrange("p l j -> p (l j)").bitcast(I32))
+        wo_w = keep.tile([P, PASSES, 2 * N], U8, align_bytes=64)
+        nc.sync.dma_start(wo_w[:].bitcast(I32), wo_words.rearrange("a p c -> p a c").bitcast(I32))
         gate_w = keep.tile([P, J], F32, align_bytes=64, tag="early_late")
         nc.sync.dma_start(gate_w[:], wgo)
+        bias = keep.tile([P, 4], F32)
+        nc.sync.dma_start(bias[:], b.rearrange("(p t) -> p t", t=4))
         node_sc = (got_sc, got_sc1)
 
         pages = {}
@@ -268,6 +267,6 @@ def tile_list_rgg_ownsiluP_kernel(tc, tab_words, tab_scales, wa_words, wa_scales
         store_codes(s2[0], s2[1])
         quantise(s3)
         store_codes(s3[0], s3[1])
-        for q in range(4):
-            queue = nc.scalar if q < 3 else nc.sync
-            queue.dma_start(out_2[0, 4 * q : 4 * q + 4, :].bitcast(I32), code_sc[32 * q : 32 * q + 4, :].bitcast(I32))
+        for r in range(4):
+            queue = nc.scalar if r < 3 else nc.sync
+            queue.dma_start(out_2[0, r:16:4, :].bitcast(I32), code_sc[r:P:32, :].bitcast(I32))

@@ -99,8 +99,7 @@ def tile_list_rgg_ownsiluP_kernel(tc, tab_words, tab_scales, wa_words, wa_scales
         def quantise_wc(a, half):
             cols = slice(half * N // 2, (half + 1) * N // 2)
             wc_bf = keep.tile([P, N // 2, 4], BF16, align_bytes=64, name="wc_bf", tag="stage%d" % (2 * a + half))
-            nc.scalar.copy(wc_bf[:].rearrange("p (c e) i -> p c i e", e=2),
-                           wc_raw[a, half].rearrange("p i (c e) -> p c i e", e=2))
+            nc.scalar.copy(wc_bf[:], wc_raw[a, half].rearrange("p i c -> p c i"))
             nc.vector.quantize_mx(wc_w[:, a, cols].bitcast(FP8X4), wc_sc[:, a, cols], wc_bf[:].rearrange("p n i -> p (n i)"))
 
         def gather_words(piece, tag):
@@ -230,7 +229,7 @@ def tile_list_rgg_ownsiluP_kernel(tc, tab_words, tab_scales, wa_words, wa_scales
 
         def weave(copy, chunk):
             words = pairs[chunk][:].rearrange("p h c e -> p h (c e)").bitcast(F32)
-            copy(woven[chunk][:].bitcast(F32).rearrange("p (c e) h -> p c h e", e=2), words.rearrange("p h (c e) -> p c h e", e=2))
+            copy(woven[chunk][:].bitcast(F32), words.rearrange("p h c -> p c h"))
 
         def quantise(chunk):
             cols = slice(chunk[0], chunk[1])

@@ -89,7 +89,7 @@ def tile_list_rgg_ownsiluP_kernel(tc, tab_words, tab_scales, wa_words, wa_scales
 
         def clear_page(t, tag, engine):
             page = keep.tile([P, T], F32, align_bytes=64, name="page%d" % t, tag=tag)
-            engine.memset(page[:], 0.0)
+            engine.memset(page[:].bitcast(I32), 0)
             pages[t] = page
 
         wc_w = keep.tile([P, PASSES, N], U32, align_bytes=64)
@@ -200,7 +200,6 @@ def tile_list_rgg_ownsiluP_kernel(tc, tab_words, tab_scales, wa_words, wa_scales
         job(1, 2, 4)
         multiply(5)
         job(2, 2, 4)
-        job(3, 0, 4)
         multiply(6)
         job(0, 4, 6)
         multiply(7)
@@ -208,7 +207,9 @@ def tile_list_rgg_ownsiluP_kernel(tc, tab_words, tab_scales, wa_words, wa_scales
         job(0, 6, 8)
         job(1, 6, 8)
         job(2, 4, 8)
-        job(3, 4, 8)
+        turn(3, 0, 4)
+        turn(3, 4, 8)
+        place(3, 0, 8)
 
         out_rows = out_0.rearrange("(p t) c -> p t c", t=4)
         for t in range(4):

@@ -109,19 +109,21 @@ def tile_list_rgg_ownsiluP_kernel(tc, tab_words, tab_scales, wa_words, wa_scales
                 nc.vector.tensor_copy(got_w[:, side, :],
                                       tab_w[:].bitcast(U32).indirect(lists[side][:, first // 16 : (first + PIECE) // 16]))
             parted = keep.tile([P, 2, PASSES, 2 * PIECE], U8, align_bytes=64, name="parted%d" % piece)
-            nc.vector.tensor_copy(parted[:].bitcast(U16), got_w[:].bitcast(U16).rearrange("p l (j a) -> p l a j", a=2))
+            for side in (DST, SRC):
+                nc.vector.tensor_copy(parted[:, side].bitcast(U16), got_w[:, side].bitcast(U16).rearrange("p (j a) -> p a j", a=2))
             for j in range(first // P, (first + PIECE) // P):
                 node_w[j] = (parted, j * P - first)
 
         clear_page(0, "page0", nc.vector)
         gather_words(0, "got0")
-        gather_words(1, "got1")
         for a in range(PASSES):
             quantise_wc(a, 0)
             quantise_wc(a, 1)
-        gather_words(2, "stage1")
+        gather_words(1, "stage1")
+        gather_words(2, "stage3")
 
-        terms = {}
+        owns = {}
+        msgs = {}
 
         def product(acc, j, side, a, w, w_scale, start, stop):
             parted, col = node_w[j]
@@ -134,85 +136,87 @@ def tile_list_rgg_ownsiluP_kernel(tc, tab_words, tab_scales, wa_words, wa_scales
 
         sums = {}
 
-        def run_pass(j, a):
+        def gate_and_message(j, a):
             if a == 0:
                 za = psum.tile([P, N], F32)
-                ow = psum.tile([P, N], F32)
                 ms = psum.tile([P, N], F32)
-                sums[j] = (za, ow, ms)
-            za, ow, ms = sums[j]
+                sums[j] = (za, ms)
+            za, ms = sums[j]
             last = a == PASSES - 1
             product(za, j, DST, a, wa_w[:, a, :].bitcast(FP4X4), w_sc[:, 0, a, :], a == 0, False)
             product(za, j, SRC, a, wb_w[:, a, :].bitcast(FP8X4), w_sc[:, 1, a, :], False, last)
-            product(ow, j, DST, a, wo_w[:, a, :].bitcast(FP4X4), w_sc[:, 2, a, :], a == 0, last)
             product(ms, j, SRC, a, wc_w[:, a, :].bitcast(FP8X4), wc_sc[:, a, :], a == 0, last)
+
+        def own_term(j):
+            ow = psum.tile([P, N], F32)
+            for a in range(PASSES):
+                product(ow, j, DST, a, wo_w[:, a, :].bitcast(FP4X4), w_sc[:, 2, a, :], a == 0, a == PASSES - 1)
+            own2 = keep.tile([P, 4, P], F32, name="own%d" % j)
+            nc.scalar.activation(own2[:], dealt(ow[:]), ACT.Copy, scale=2.0)
+            owns[j] = own2
 
         def multiply(j):
             for a in range(PASSES):
-                run_pass(j, a)
+                gate_and_message(j, a)
             combine(j)
+            own_term(j)
 
         def combine(j):
-            za, ow, ms = sums[j]
+            za, ms = sums[j]
             th = keep.tile([P, 4, P], F32, align_bytes=64, name="th", tag="th%d" % j)
             nc.scalar.activation(th[:], dealt(za[:]), ACT.Tanh, scale=0.5)
-            own2 = keep.tile([P, 4, P], F32, name="own%d" % j)
-            nc.scalar.activation(own2[:], dealt(ow[:]), ACT.Copy, scale=2.0)
             msg2 = keep.tile([P, 4, P], F32, name="msg%d" % j)
             nc.vector.scalar_tensor_tensor(msg2[:], th[:], 1.0, dealt(ms[:]), ALU.add, ALU.mult)
-            terms[j] = (own2, msg2)
+            msgs[j] = msg2
 
-        acts = [keep.tile([P, J], F32, name="act%d" % t) for t in range(4)]
-
-        def turn(t, lo, hi):
+        def turn(t, lo, hi, act):
             turned = psum.tile([P, 4, P], F32)
             for j in range(lo, hi):
-                own2, msg2 = terms[j]
-                nc.tensor.matmul(turned[:, j - lo, :], lhsT=own2[:, t, :], rhs=ident[:], start=True, stop=False, is_transpose=True)
-                nc.tensor.matmul(turned[:, j - lo, :], lhsT=msg2[:, t, :], rhs=ident[:], start=False, stop=True, is_transpose=True)
-            nc.scalar.activation(acts[t][:, lo * P : hi * P], turned[:, 0 : hi - lo, :].rearrange("p j m -> p (j m)"),
+                nc.tensor.matmul(turned[:, j - lo, :], lhsT=owns[j][:, t, :], rhs=ident[:], start=True, stop=False, is_transpose=True)
+                nc.tensor.matmul(turned[:, j - lo, :], lhsT=msgs[j][:, t, :], rhs=ident[:], start=False, stop=True, is_transpose=True)
+            nc.scalar.activation(act, turned[:, 0 : hi - lo, :].rearrange("p j m -> p (j m)"),
                                  ACT.Silu, bias=bias[:, t : t + 1], scale=0.5)
 
-        def place(t, lo, hi):
-            cols = slice(lo * P, hi * P)
-            nc.vector.tensor_tensor(pages[t][:].indirect(lists[DST][:, lo * 8 : hi * 8]), acts[t][:, cols], gate_w[:, cols], ALU.mult)
-
-        def job(t, lo, hi):
-            turn(t, lo, hi)
-            place(t, lo, hi)
+        def job(t, lo, hi, tag):
+            act = keep.tile([P, (hi - lo) * P], F32, name="act", tag=tag)
+            banks = -(-(hi - lo) // 4)
+            step = (hi - lo) // banks
+            for first in range(lo, hi, step):
+                turn(t, first, first + step, act[:, (first - lo) * P : (first - lo + step) * P])
+            nc.vector.tensor_tensor(pages[t][:].indirect(lists[DST][:, lo * 8 : hi * 8]), act[:], gate_w[:, lo * P : hi * P], ALU.mult)
 
         for a in range(PASSES):
-            run_pass(0, a)
-            run_pass(1, a)
+            gate_and_message(0, a)
+            gate_and_message(1, a)
         combine(0)
         combine(1)
+        own_term(0)
+        own_term(1)
         gather_words(3, "th1")
         clear_page(1, "th1", nc.gpsimd)
-        job(0, 0, 2)
-        job(1, 0, 2)
+        job(0, 0, 2, "act0_0")
+        job(1, 0, 2, "act1_0")
         multiply(2)
         clear_page(2, "th2", nc.gpsimd)
         multiply(3)
         clear_page(3, "th3", nc.gpsimd)
-        job(2, 0, 2)
+        job(2, 0, 2, "act2_0")
         multiply(4)
-        job(0, 2, 4)
-        job(1, 2, 4)
+        job(0, 2, 4, "act0_2")
+        job(1, 2, 4, "act1_2")
         multiply(5)
-        job(2, 2, 4)
+        job(2, 2, 4, "act2_2")
         multiply(6)
-        job(0, 4, 6)
+        job(0, 4, 6, "act0_4")
         multiply(7)
-        job(1, 4, 6)
-        job(0, 6, 8)
-        job(1, 6, 8)
-        job(2, 4, 8)
-        turn(3, 0, 4)
-        turn(3, 4, 8)
-        place(3, 0, 8)
+        job(1, 4, 6, "act1_4")
+        job(0, 6, 8, "act0_6")
+        job(1, 6, 8, "act1_6")
+        job(2, 4, 8, "act2_4")
+        job(3, 0, 6, "act3_0")
 
         out_rows = out_0.rearrange("(p t) c -> p t c", t=4)
-        for t in range(4):
+        for t in range(3):
             nc.sync.dma_start(out_rows[:, t, :], pages[t][:])
 
         pairs = {}
@@ -239,30 +243,32 @@ def tile_list_rgg_ownsiluP_kernel(tc, tab_words, tab_scales, wa_words, wa_scales
         def store_codes(lo, hi):
             nc.sync.dma_start(out_words[:, lo:hi], codes[:, lo:hi].bitcast(I32))
 
-        for t in range(2):
-            for chunk in VECTOR_CHUNKS + SCALAR_CHUNKS:
+        for chunk in VECTOR_CHUNKS + SCALAR_CHUNKS:
+            round_page(nc.scalar.copy, 0, chunk)
+        for t in (1, 2):
+            for chunk in VECTOR_CHUNKS:
                 round_page(nc.scalar.copy, t, chunk)
-        for chunk in SCALAR_CHUNKS:
-            round_page(nc.scalar.copy, 2, chunk)
+        job(3, 6, 8, "act2_4")
+        nc.sync.dma_start(out_rows[:, 3, :], pages[3][:])
+        for t in (1, 2):
+            for chunk in SCALAR_CHUNKS:
+                round_page(nc.scalar.copy, t, chunk)
         for chunk in SCALAR_CHUNKS:
             round_page(nc.scalar.copy, 3, chunk)
             weave(nc.scalar.copy, chunk)
         va, vb = VECTOR_CHUNKS
         s0, s1, s2, s3 = SCALAR_CHUNKS
         vcopy = nc.vector.tensor_copy
-        round_page(vcopy, 2, va)
         round_page(vcopy, 3, va)
-        round_page(vcopy, 2, vb)
-        weave(vcopy, va)
         round_page(vcopy, 3, vb)
-        quantise(va)
-        store_codes(va[0], va[1])
+        weave(vcopy, va)
         weave(vcopy, vb)
+        quantise(va)
         quantise(s0)
+        quantise(vb)
+        store_codes(va[0], vb[1])
         quantise(s1)
         store_codes(s0[0], s1[1])
-        quantise(vb)
-        store_codes(vb[0], vb[1])
         quantise(s2)
         store_codes(s2[0], s2[1])
         quantise(s3)

@@ -49,7 +49,7 @@ def tile_list_rgg_ownsiluP_kernel(tc, tab_words, tab_scales, wa_words, wa_scales
             wc_pass = keep.tile([P, 4, N], F32, name="wc_pass%d" % a)
             nc.sync.dma_start(wc_pass[:], wc_rows[a])
             for half in range(2):
-                wc_raw[a, half] = wc_pass[:, :, half * N // 2 : (half + 1) * N // 2]
+                wc_raw[a, half] = wc_pass[:].rearrange("p i (m h t) -> p h m i t", h=2, t=2)[:, half]
 
         load_wc(0)
         w_sc_rows = keep.tile([16, 3, PASSES, N], U8, align_bytes=64)
@@ -99,7 +99,7 @@ def tile_list_rgg_ownsiluP_kernel(tc, tab_words, tab_scales, wa_words, wa_scales
         def quantise_wc(a, half):
             cols = slice(half * N // 2, (half + 1) * N // 2)
             wc_bf = keep.tile([P, N // 2, 4], BF16, align_bytes=64, name="wc_bf", tag="stage%d" % (2 * a + half))
-            nc.scalar.copy(wc_bf[:], wc_raw[a, half].rearrange("p i c -> p c i"))
+            nc.scalar.copy(wc_bf[:].rearrange("p (t m) i -> p m i t", t=2), wc_raw[a, half])
             nc.vector.quantize_mx(wc_w[:, a, cols].bitcast(FP8X4), wc_sc[:, a, cols], wc_bf[:].rearrange("p n i -> p (n i)"))
 
         def gather_words(piece, tag):
@@ -131,8 +131,11 @@ def tile_list_rgg_ownsiluP_kernel(tc, tab_words, tab_scales, wa_words, wa_scales
                                 lhsT_scale=node_sc[a][:, side, j * P : (j + 1) * P],
                                 rhs=w, rhs_scale=w_scale, start=start, stop=stop)
 
-        def dealt(ap):
-            return ap.rearrange("p (m t) -> p t m", t=4)
+        def by_channel(bank):
+            return bank[:].rearrange("p (m t) -> p m t", t=4)
+
+        def dealt(tile):
+            return tile[:].rearrange("p t m -> p m t")
 
         sums = {}
 
@@ -152,7 +155,7 @@ def tile_list_rgg_ownsiluP_kernel(tc, tab_words, tab_scales, wa_words, wa_scales
             for a in range(PASSES):
                 product(ow, j, DST, a, wo_w[:, a, :].bitcast(FP4X4), w_sc[:, 2, a, :], a == 0, a == PASSES - 1)
             own2 = keep.tile([P, 4, P], F32, name="own%d" % j)
-            nc.scalar.activation(own2[:], dealt(ow[:]), ACT.Copy, scale=2.0)
+            nc.scalar.activation(dealt(own2), by_channel(ow), ACT.Copy, scale=2.0)
             owns[j] = own2
 
         def multiply(j):
@@ -164,9 +167,9 @@ def tile_list_rgg_ownsiluP_kernel(tc, tab_words, tab_scales, wa_words, wa_scales
         def combine(j):
             za, ms = sums[j]
             th = keep.tile([P, 4, P], F32, align_bytes=64, name="th", tag="th%d" % j)
-            nc.scalar.activation(th[:], dealt(za[:]), ACT.Tanh, scale=0.5)
+            nc.scalar.activation(dealt(th), by_channel(za), ACT.Tanh, scale=0.5)
             msg2 = keep.tile([P, 4, P], F32, name="msg%d" % j)
-            nc.vector.scalar_tensor_tensor(msg2[:], th[:], 1.0, dealt(ms[:]), ALU.add, ALU.mult)
+            nc.vector.scalar_tensor_tensor(msg2[:], th[:], 1.0, ms[:].rearrange("p (t m) -> p t m", t=4), ALU.add, ALU.mult)
             msgs[j] = msg2
 
         def turn(t, lo, hi, act):

@@ -38,7 +38,7 @@ def tile_list_rgg_ownsiluP_kernel(tc, tab_words, tab_scales, wa_words, wa_scales
         nc.gpsimd.memset(tab_sc[:].bitcast(I32), 0)
         nc.sync.dma_start(lists[DST][:], offs2)
         nc.sync.dma_start(lists[SRC][:], offs)
-        for q in range(4):
+        for q in (0, 2, 1, 3):
             nc.sync.dma_start(tab_sc[32 * q : 32 * q + 8, :].bitcast(I32), tab_scales[:, 4 * q : 4 * q + 4, :].bitcast(I32))
         tab_w = keep.tile([P, T], I32, align_bytes=64)
         nc.sync.dma_start(tab_w[:], tab_words[0].rearrange("p t i -> p (t i)").bitcast(I32))
@@ -181,7 +181,7 @@ def tile_list_rgg_ownsiluP_kernel(tc, tab_words, tab_scales, wa_words, wa_scales
                                  ACT.Silu, bias=bias[:, t : t + 1], scale=0.5)
 
         def job(t, lo, hi, tag):
-            act = keep.tile([P, (hi - lo) * P], F32, name="act", tag=tag)
+            act = keep.tile([P, (hi - lo) * P], F32, align_bytes=64, name="act", tag=tag)
             banks = -(-(hi - lo) // 4)
             step = (hi - lo) // banks
             for first in range(lo, hi, step):
@@ -198,12 +198,13 @@ def tile_list_rgg_ownsiluP_kernel(tc, tab_words, tab_scales, wa_words, wa_scales
         gather_words(3, "th1")
         clear_page(1, "th1", nc.gpsimd)
         job(0, 0, 2, "act0_0")
+        clear_page(2, "act0_0", nc.gpsimd)
         job(1, 0, 2, "act1_0")
+        clear_page(3, "act1_0", nc.gpsimd)
         multiply(2)
-        clear_page(2, "th2", nc.gpsimd)
         multiply(3)
-        clear_page(3, "th3", nc.gpsimd)
         job(2, 0, 2, "act2_0")
+        job(3, 0, 2, "act3_0")
         multiply(4)
         job(0, 2, 4, "act0_2")
         job(1, 2, 4, "act1_2")
@@ -216,7 +217,7 @@ def tile_list_rgg_ownsiluP_kernel(tc, tab_words, tab_scales, wa_words, wa_scales
         job(0, 6, 8, "act0_6")
         job(1, 6, 8, "act1_6")
         job(2, 4, 8, "act2_4")
-        job(3, 0, 6, "act3_0")
+        job(3, 2, 6, "act3_2")
 
         out_rows = out_0.rearrange("(p t) c -> p t c", t=4)
         for t in range(3):
@@ -248,9 +249,10 @@ def tile_list_rgg_ownsiluP_kernel(tc, tab_words, tab_scales, wa_words, wa_scales
 
         for chunk in VECTOR_CHUNKS + SCALAR_CHUNKS:
             round_page(nc.scalar.copy, 0, chunk)
-        for t in (1, 2):
-            for chunk in VECTOR_CHUNKS:
-                round_page(nc.scalar.copy, t, chunk)
+        va, vb = VECTOR_CHUNKS
+        round_page(nc.scalar.copy, 1, va)
+        round_page(nc.scalar.copy, 1, vb)
+        round_page(nc.scalar.copy, 2, va)
         job(3, 6, 8, "act2_4")
         nc.sync.dma_start(out_rows[:, 3, :], pages[3][:])
         for t in (1, 2):
@@ -259,14 +261,14 @@ def tile_list_rgg_ownsiluP_kernel(tc, tab_words, tab_scales, wa_words, wa_scales
         for chunk in SCALAR_CHUNKS:
             round_page(nc.scalar.copy, 3, chunk)
             weave(nc.scalar.copy, chunk)
-        va, vb = VECTOR_CHUNKS
         s0, s1, s2, s3 = SCALAR_CHUNKS
         vcopy = nc.vector.tensor_copy
         round_page(vcopy, 3, va)
-        round_page(vcopy, 3, vb)
+        round_page(vcopy, 2, vb)
         weave(vcopy, va)
-        weave(vcopy, vb)
+        round_page(vcopy, 3, vb)
         quantise(va)
+        weave(vcopy, vb)
         quantise(s0)
         quantise(vb)
         store_codes(va[0], vb[1])

@@ -24,6 +24,7 @@ PIECE = 256
 VECTOR_CHUNKS = ((0, 512), (512, 1024))
 SCALAR_CHUNKS = ((1024, 1280), (1280, 1536), (1536, 1792), (1792, 2048))
 SRC, DST = 0, 1
+GPSIMD_TILES = (5, 6, 7)
 
 
 def tile_list_rgg_ownsiluP_kernel(tc, tab_words, tab_scales, wa_words, wa_scales, wb_words, wb_scales, wc,
@@ -154,7 +155,7 @@ def tile_list_rgg_ownsiluP_kernel(tc, tab_words, tab_scales, wa_words, wa_scales
             ow = psum.tile([P, N], F32)
             for a in range(PASSES):
                 product(ow, j, DST, a, wo_w[:, a, :].bitcast(FP4X4), w_sc[:, 2, a, :], a == 0, a == PASSES - 1)
-            own2 = keep.tile([P, 4, P], F32, name="own%d" % j)
+            own2 = keep.tile([P, 4, P], F32, align_bytes=64, name="own", tag="own%d" % j)
             nc.scalar.activation(dealt(own2), by_channel(ow), ACT.Copy, scale=2.0)
             owns[j] = own2
 
@@ -168,25 +169,39 @@ def tile_list_rgg_ownsiluP_kernel(tc, tab_words, tab_scales, wa_words, wa_scales
             za, ms = sums[j]
             th = keep.tile([P, 4, P], F32, align_bytes=64, name="th", tag="th%d" % j)
             nc.scalar.activation(dealt(th), by_channel(za), ACT.Tanh, scale=0.5)
-            msg2 = keep.tile([P, 4, P], F32, name="msg%d" % j)
-            nc.vector.scalar_tensor_tensor(msg2[:], th[:], 1.0, ms[:].rearrange("p (t m) -> p t m", t=4), ALU.add, ALU.mult)
-            msgs[j] = msg2
+            msg2 = keep.tile([P, 4, P], F32, align_bytes=64, name="msg", tag="msg%d" % j)
+            msgs[j] = [msg2]
+            if j in GPSIMD_TILES:
+                plain = keep.tile([P, 4, P], F32, name="plain%d" % j)
+                nc.scalar.copy(plain[:], ms[:].rearrange("p (t m) -> p t m", t=4))
+                nc.gpsimd.tensor_tensor(msg2[:], th[:], plain[:], ALU.mult)
+                msgs[j].append(plain)
+            else:
+                nc.vector.scalar_tensor_tensor(msg2[:], th[:], 1.0, ms[:].rearrange("p (t m) -> p t m", t=4), ALU.add, ALU.mult)
 
         def turn(t, lo, hi, act):
             turned = psum.tile([P, 4, P], F32)
             for j in range(lo, hi):
-                nc.tensor.matmul(turned[:, j - lo, :], lhsT=owns[j][:, t, :], rhs=ident[:], start=True, stop=False, is_transpose=True)
-                nc.tensor.matmul(turned[:, j - lo, :], lhsT=msgs[j][:, t, :], rhs=ident[:], start=False, stop=True, is_transpose=True)
+                terms = [owns[j]] + msgs[j][::-1]
+                for n, term in enumerate(terms):
+                    nc.tensor.matmul(turned[:, j - lo, :], lhsT=term[:, t, :], rhs=ident[:], start=n == 0, stop=n == len(terms) - 1,
+                                     is_transpose=True)
             nc.scalar.activation(act, turned[:, 0 : hi - lo, :].rearrange("p j m -> p (j m)"),
                                  ACT.Silu, bias=bias[:, t : t + 1], scale=0.5)
 
-        def job(t, lo, hi, tag):
+        def job(t, lo, hi, tag, fused=True):
             act = keep.tile([P, (hi - lo) * P], F32, align_bytes=64, name="act", tag=tag)
             banks = -(-(hi - lo) // 4)
             step = (hi - lo) // banks
             for first in range(lo, hi, step):
                 turn(t, first, first + step, act[:, (first - lo) * P : (first - lo + step) * P])
-            nc.vector.tensor_tensor(pages[t][:].indirect(lists[DST][:, lo * 8 : hi * 8]), act[:], gate_w[:, lo * P : hi * P], ALU.mult)
+            window = pages[t][:].indirect(lists[DST][:, lo * 8 : hi * 8])
+            if fused:
+                nc.vector.tensor_tensor(window, act[:], gate_w[:, lo * P : hi * P], ALU.mult)
+            else:
+                weighted = keep.tile([P, (hi - lo) * P], F32, align_bytes=64, name="weighted%d_%d" % (t, lo))
+                nc.gpsimd.tensor_tensor(weighted[:], act[:], gate_w[:, lo * P : hi * P], ALU.mult)
+                nc.vector.tensor_copy(window, weighted[:])
 
         for a in range(PASSES):
             gate_and_message(0, a)
@@ -206,17 +221,18 @@ def tile_list_rgg_ownsiluP_kernel(tc, tab_words, tab_scales, wa_words, wa_scales
         job(2, 0, 2, "act2_0")
         job(3, 0, 2, "act3_0")
         multiply(4)
-        job(0, 2, 4, "act0_2")
-        job(1, 2, 4, "act1_2")
+        job(0, 2, 4, "act0_2", False)
+        job(1, 2, 4, "act1_2", False)
         multiply(5)
-        job(2, 2, 4, "act2_2")
+        job(2, 2, 4, "act2_2", False)
         multiply(6)
-        job(0, 4, 6, "act0_4")
+        job(0, 4, 6, "act0_4", False)
+        job(1, 4, 6, "act1_4", False)
         multiply(7)
-        job(1, 4, 6, "act1_4")
+        job(2, 4, 6, "act2_4", False)
         job(0, 6, 8, "act0_6")
         job(1, 6, 8, "act1_6")
-        job(2, 4, 8, "act2_4")
+        job(2, 6, 8, "act2_6")
         job(3, 2, 6, "act3_2")
 
         out_rows = out_0.rearrange("(p t) c -> p t c", t=4)
@@ -225,9 +241,9 @@ def tile_list_rgg_ownsiluP_kernel(tc, tab_words, tab_scales, wa_words, wa_scales
 
         pairs = {}
         woven = {}
-        for chunk in VECTOR_CHUNKS + SCALAR_CHUNKS:
+        for chunk, tag in zip(VECTOR_CHUNKS + SCALAR_CHUNKS, ("msg5", "own5", "msg4", "own4", "msg3", "own3")):
             lo, hi = chunk
-            pairs[chunk] = keep.tile([P, 2, hi - lo, 2], BF16, align_bytes=64, name="pairs%d" % lo)
+            pairs[chunk] = keep.tile([P, 2, hi - lo, 2], BF16, align_bytes=64, name="pairs", tag=tag)
             woven[chunk] = keep.tile([P, hi - lo, 4], BF16, align_bytes=64, name="woven%d" % lo)
         codes = keep.tile([P, T], U32, align_bytes=64)
         code_sc = keep.tile([P, T], U8, align_bytes=64)
@@ -253,7 +269,7 @@ def tile_list_rgg_ownsiluP_kernel(tc, tab_words, tab_scales, wa_words, wa_scales
         round_page(nc.scalar.copy, 1, va)
         round_page(nc.scalar.copy, 1, vb)
         round_page(nc.scalar.copy, 2, va)
-        job(3, 6, 8, "act2_4")
+        job(3, 6, 8, "act2_6")
         nc.sync.dma_start(out_rows[:, 3, :], pages[3][:])
         for t in (1, 2):
             for chunk in SCALAR_CHUNKS:

@@ -159,10 +159,13 @@ def tile_list_rgg_ownsiluP_kernel(tc, tab_words, tab_scales, wa_words, wa_scales
             nc.scalar.activation(dealt(own2), by_channel(ow), ACT.Copy, scale=2.0)
             owns[j] = own2
 
-        def multiply(j):
+        def gated_message(j):
             for a in range(PASSES):
                 gate_and_message(j, a)
             combine(j)
+
+        def multiply(j):
+            gated_message(j)
             own_term(j)
 
         def combine(j):
@@ -174,7 +177,8 @@ def tile_list_rgg_ownsiluP_kernel(tc, tab_words, tab_scales, wa_words, wa_scales
             if j in GPSIMD_TILES:
                 plain = keep.tile([P, 4, P], F32, name="plain%d" % j)
                 nc.scalar.copy(plain[:], ms[:].rearrange("p (t m) -> p t m", t=4))
-                nc.gpsimd.tensor_tensor(msg2[:], th[:], plain[:], ALU.mult)
+                for part in ((slice(0, 1), slice(1, 4)) if j % 2 else (slice(0, 4),)):
+                    nc.gpsimd.tensor_tensor(msg2[:, part], th[:, part], plain[:, part], ALU.mult)
                 msgs[j].append(plain)
             else:
                 nc.vector.scalar_tensor_tensor(msg2[:], th[:], 1.0, ms[:].rearrange("p (t m) -> p t m", t=4), ALU.add, ALU.mult)
@@ -225,11 +229,13 @@ def tile_list_rgg_ownsiluP_kernel(tc, tab_words, tab_scales, wa_words, wa_scales
         job(1, 2, 4, "act1_2", False)
         multiply(5)
         job(2, 2, 4, "act2_2", False)
-        multiply(6)
         job(0, 4, 6, "act0_4", False)
+        gated_message(6)
         job(1, 4, 6, "act1_4", False)
-        multiply(7)
         job(2, 4, 6, "act2_4", False)
+        gated_message(7)
+        own_term(6)
+        own_term(7)
         job(0, 6, 8, "act0_6")
         job(1, 6, 8, "act1_6")
         job(2, 6, 8, "act2_6")

@@ -69,6 +69,8 @@ def tile_list_rgg_ownsiluP_kernel(tc, tab_words, tab_scales, wa_words, wa_scales
 
         ident = keep.tile([P, P], F32)
         make_identity(nc, ident[:])
+        warm = keep.tile([P, 1], F32)
+        nc.scalar.activation(warm[:], ident[:, 0:1], ACT.Silu)
 
         got_sc = keep.tile([P, 2, J], U8, align_bytes=64)
         got_sc1 = keep.tile([P, 2, J], U8, align_bytes=64)
@@ -116,6 +118,7 @@ def tile_list_rgg_ownsiluP_kernel(tc, tab_words, tab_scales, wa_words, wa_scales
                 node_w[j] = (parted, j * P - first)
 
         clear_page(0, "page0", nc.vector)
+        clear_page(1, "page1", nc.vector)
         gather_words(0, "got0")
         for a in range(PASSES):
             quantise_wc(a, 0)
@@ -140,16 +143,19 @@ def tile_list_rgg_ownsiluP_kernel(tc, tab_words, tab_scales, wa_words, wa_scales
 
         sums = {}
 
-        def gate_and_message(j, a):
-            if a == 0:
-                za = psum.tile([P, N], F32)
-                ms = psum.tile([P, N], F32)
-                sums[j] = (za, ms)
-            za, ms = sums[j]
-            last = a == PASSES - 1
-            product(za, j, DST, a, wa_w[:, a, :].bitcast(FP4X4), w_sc[:, 0, a, :], a == 0, False)
-            product(za, j, SRC, a, wb_w[:, a, :].bitcast(FP8X4), w_sc[:, 1, a, :], False, last)
-            product(ms, j, SRC, a, wc_w[:, a, :].bitcast(FP8X4), wc_sc[:, a, :], a == 0, last)
+        def open_sums(j):
+            za = psum.tile([P, N], F32)
+            ms = psum.tile([P, N], F32)
+            sums[j] = (za, ms)
+
+        def target_pass(j, a):
+            product(sums[j][0], j, DST, a, wa_w[:, a, :].bitcast(FP4X4), w_sc[:, 0, a, :], a == 0, False)
+
+        def source_pass(j, a):
+            product(sums[j][0], j, SRC, a, wb_w[:, a, :].bitcast(FP8X4), w_sc[:, 1, a, :], False, a == PASSES - 1)
+
+        def message_pass(j, a):
+            product(sums[j][1], j, SRC, a, wc_w[:, a, :].bitcast(FP8X4), wc_sc[:, a, :], a == 0, a == PASSES - 1)
 
         def own_term(j):
             ow = psum.tile([P, N], F32)
@@ -160,8 +166,11 @@ def tile_list_rgg_ownsiluP_kernel(tc, tab_words, tab_scales, wa_words, wa_scales
             owns[j] = own2
 
         def gated_message(j):
+            open_sums(j)
             for a in range(PASSES):
-                gate_and_message(j, a)
+                target_pass(j, a)
+                source_pass(j, a)
+                message_pass(j, a)
             combine(j)
 
         def multiply(j):
@@ -207,19 +216,25 @@ def tile_list_rgg_ownsiluP_kernel(tc, tab_words, tab_scales, wa_words, wa_scales
                 nc.gpsimd.tensor_tensor(weighted[:], act[:], gate_w[:, lo * P : hi * P], ALU.mult)
                 nc.vector.tensor_copy(window, weighted[:])
 
-        for a in range(PASSES):
-            gate_and_message(0, a)
-            gate_and_message(1, a)
+        open_sums(0)
+        open_sums(1)
+        for step in (target_pass, message_pass, source_pass):
+            step(0, 0)
+            step(1, 0)
+        for j in (0, 1):
+            target_pass(j, 1)
+            source_pass(j, 1)
+        message_pass(0, 1)
+        message_pass(1, 1)
         combine(0)
         combine(1)
         own_term(0)
         own_term(1)
         gather_words(3, "th1")
-        clear_page(1, "th1", nc.gpsimd)
+        clear_page(2, "th1", nc.gpsimd)
         job(0, 0, 2, "act0_0")
-        clear_page(2, "act0_0", nc.gpsimd)
+        clear_page(3, "act0_0", nc.gpsimd)
         job(1, 0, 2, "act1_0")
-        clear_page(3, "act1_0", nc.gpsimd)
         multiply(2)
         multiply(3)
         job(2, 0, 2, "act2_0")

@@ -73,16 +73,15 @@ def tile_list_rgg_ownsiluP_kernel(tc, tab_words, tab_scales, wa_words, wa_scales
         nc.scalar.activation(warm[:], ident[:, 0:1], ACT.Silu)
 
         got_sc = keep.tile([P, 2, J], U8, align_bytes=64)
-        got_sc1 = keep.tile([P, 2, J], U8, align_bytes=64)
-        nc.vector.memset(got_sc1[:].rearrange("p l j -> p (l j)").bitcast(I32), 0)
         for side in (DST, SRC):
             nc.vector.tensor_copy(got_sc[:, side, :], tab_sc[:].indirect(lists[side][:]))
+        got_sc1 = keep.tile([P, 2, J], U8, align_bytes=64, tag="early_late")
         for r in range(4):
             nc.sync.dma_start(got_sc1[r:P:32].rearrange("p l j -> p (l j)").bitcast(I32),
                               got_sc[4 + r : P : 32].rearrange("p l j -> p (l j)").bitcast(I32))
         wo_w = keep.tile([P, PASSES, 2 * N], U8, align_bytes=64)
         nc.sync.dma_start(wo_w[:].bitcast(I32), wo_words.rearrange("a p c -> p a c").bitcast(I32))
-        gate_w = keep.tile([P, J], F32, align_bytes=64, tag="early_late")
+        gate_w = keep.tile([P, J], F32, tag="w_sc_rows", align_bytes=64)
         nc.sync.dma_start(gate_w[:], wgo)
         bias = keep.tile([P, 4], F32)
         nc.sync.dma_start(bias[:], b.rearrange("(p t) -> p t", t=4))
@@ -267,7 +266,7 @@ def tile_list_rgg_ownsiluP_kernel(tc, tab_words, tab_scales, wa_words, wa_scales
             pairs[chunk] = keep.tile([P, 2, hi - lo, 2], BF16, align_bytes=64, name="pairs", tag=tag)
             woven[chunk] = keep.tile([P, hi - lo, 4], BF16, align_bytes=64, name="woven%d" % lo)
         codes = keep.tile([P, T], U32, align_bytes=64)
-        code_sc = keep.tile([P, T], U8, align_bytes=64)
+        code_sc = keep.tile([P, T // 2], U8, align_bytes=64)
         out_words = out_1[0].rearrange("p t i -> p (t i)").bitcast(I32)
 
         def round_page(copy, t, chunk):
@@ -279,7 +278,9 @@ def tile_list_rgg_ownsiluP_kernel(tc, tab_words, tab_scales, wa_words, wa_scales
 
         def quantise(chunk):
             cols = slice(chunk[0], chunk[1])
-            nc.vector.quantize_mx(codes[:, cols].bitcast(FP8X4), code_sc[:, cols], woven[chunk][:].rearrange("p c i -> p (c i)"))
+            half, first = divmod(chunk[0], T // 2)
+            plane = code_sc[4 * half :, first : first + chunk[1] - chunk[0]]
+            nc.vector.quantize_mx(codes[:, cols].bitcast(FP8X4), plane, woven[chunk][:].rearrange("p c i -> p (c i)"))
 
         def store_codes(lo, hi):
             nc.sync.dma_start(out_words[:, lo:hi], codes[:, lo:hi].bitcast(I32))
@@ -315,6 +316,7 @@ def tile_list_rgg_ownsiluP_kernel(tc, tab_words, tab_scales, wa_words, wa_scales
         store_codes(s2[0], s2[1])
         quantise(s3)
         store_codes(s3[0], s3[1])
-        for r in range(4):
-            queue = nc.scalar if r < 3 else nc.sync
-            queue.dma_start(out_2[0, r:16:4, :].bitcast(I32), code_sc[r:P:32, :].bitcast(I32))
+        for q in (0, 2, 1, 3):
+            queue = nc.scalar if q < 3 else nc.sync
+            rows = out_2[0, 4 * q : 4 * q + 4, :].rearrange("r (h c) -> h r c", h=2)
+            queue.dma_start(rows.bitcast(I32), code_sc[32 * q : 32 * q + 8, :].bitcast(I32))

@@ -164,11 +164,16 @@ def tile_list_rgg_ownsiluP_kernel(tc, tab_words, tab_scales, wa_words, wa_scales
             nc.scalar.activation(dealt(own2), by_channel(ow), ACT.Copy, scale=2.0)
             owns[j] = own2
 
-        def gated_message(j):
+        def gate_sum(j):
             open_sums(j)
             for a in range(PASSES):
                 target_pass(j, a)
                 source_pass(j, a)
+
+        def gated_message(j):
+            if j not in sums:
+                gate_sum(j)
+            for a in range(PASSES):
                 message_pass(j, a)
             combine(j)
 
@@ -231,6 +236,7 @@ def tile_list_rgg_ownsiluP_kernel(tc, tab_words, tab_scales, wa_words, wa_scales
         own_term(1)
         gather_words(3, "th1")
         clear_page(2, "th1", nc.gpsimd)
+        gate_sum(2)
         job(0, 0, 2, "act0_0")
         clear_page(3, "act0_0", nc.gpsimd)
         job(1, 0, 2, "act1_0")

@@ -140,6 +140,9 @@ def tile_list_rgg_ownsiluP_kernel(tc, tab_words, tab_scales, wa_words, wa_scales
         def dealt(tile):
             return tile[:].rearrange("p t m -> p m t")
 
+        def slices_of(j):
+            return (slice(0, 1), slice(1, 4)) if j in GPSIMD_TILES and j % 2 else (slice(0, 4),)
+
         sums = {}
 
         def open_sums(j):
@@ -161,7 +164,8 @@ def tile_list_rgg_ownsiluP_kernel(tc, tab_words, tab_scales, wa_words, wa_scales
             for a in range(PASSES):
                 product(ow, j, DST, a, wo_w[:, a, :].bitcast(FP4X4), w_sc[:, 2, a, :], a == 0, a == PASSES - 1)
             own2 = keep.tile([P, 4, P], F32, align_bytes=64, name="own", tag="own%d" % j)
-            nc.scalar.activation(dealt(own2), by_channel(ow), ACT.Copy, scale=2.0)
+            for part in slices_of(j):
+                nc.scalar.activation(dealt(own2)[:, :, part], by_channel(ow)[:, :, part], ACT.Copy, scale=2.0)
             owns[j] = own2
 
         def gate_sum(j):
@@ -189,8 +193,9 @@ def tile_list_rgg_ownsiluP_kernel(tc, tab_words, tab_scales, wa_words, wa_scales
             msgs[j] = [msg2]
             if j in GPSIMD_TILES:
                 plain = keep.tile([P, 4, P], F32, name="plain%d" % j)
-                nc.scalar.copy(plain[:], ms[:].rearrange("p (t m) -> p t m", t=4))
-                for part in ((slice(0, 1), slice(1, 4)) if j % 2 else (slice(0, 4),)):
+                for part in slices_of(j):
+                    nc.scalar.copy(plain[:, part], ms[:].rearrange("p (t m) -> p t m", t=4)[:, part])
+                for part in slices_of(j):
                     nc.gpsimd.tensor_tensor(msg2[:, part], th[:, part], plain[:, part], ALU.mult)
                 msgs[j].append(plain)
             else:
@@ -240,18 +245,22 @@ def tile_list_rgg_ownsiluP_kernel(tc, tab_words, tab_scales, wa_words, wa_scales
         job(0, 0, 2, "act0_0")
         clear_page(3, "act0_0", nc.gpsimd)
         job(1, 0, 2, "act1_0")
-        multiply(2)
-        multiply(3)
+        gated_message(2)
+        gated_message(3)
         job(2, 0, 2, "act2_0")
         job(3, 0, 2, "act3_0")
-        multiply(4)
+        own_term(2)
+        own_term(3)
+        gated_message(4)
         job(0, 2, 4, "act0_2", False)
         job(1, 2, 4, "act1_2", False)
-        multiply(5)
+        gated_message(5)
+        own_term(4)
+        own_term(5)
         job(2, 2, 4, "act2_2", False)
         job(0, 4, 6, "act0_4", False)
-        gated_message(6)
         job(1, 4, 6, "act1_4", False)
+        gated_message(6)
         job(2, 4, 6, "act2_4", False)
         gated_message(7)
         own_term(6)

@@ -41,8 +41,6 @@ def tile_list_rgg_ownsiluP_kernel(tc, tab_words, tab_scales, wa_words, wa_scales
         nc.sync.dma_start(lists[SRC][:], offs)
         for q in (0, 2, 1, 3):
             nc.sync.dma_start(tab_sc[32 * q : 32 * q + 8, :].bitcast(I32), tab_scales[:, 4 * q : 4 * q + 4, :].bitcast(I32))
-        tab_w = keep.tile([P, T], I32, align_bytes=64)
-        nc.sync.dma_start(tab_w[:], tab_words[0].rearrange("p t i -> p (t i)").bitcast(I32))
         wc_rows = wc.rearrange("(a p i) n -> a p i n", a=PASSES, i=4)
         wc_raw = {}
 
@@ -50,15 +48,16 @@ def tile_list_rgg_ownsiluP_kernel(tc, tab_words, tab_scales, wa_words, wa_scales
             wc_pass = keep.tile([P, 4, N], F32, name="wc_pass%d" % a)
             nc.sync.dma_start(wc_pass[:], wc_rows[a])
             for half in range(2):
-                wc_raw[a, half] = wc_pass[:].rearrange("p i (m h t) -> p h m i t", h=2, t=2)[:, half]
+                wc_raw[a, half] = wc_pass[:].rearrange("p i (h c k) -> p h c i k", h=2, k=4)[:, half]
 
         load_wc(0)
+        tab_w = keep.tile([P, T], I32, align_bytes=64)
+        nc.sync.dma_start(tab_w[:], tab_words[0].rearrange("p t i -> p (t i)").bitcast(I32))
         w_sc_rows = keep.tile([16, 3, PASSES, N], U8, align_bytes=64)
         for w, scales in enumerate((wa_scales, wb_scales, wo_scales)):
             nc.sync.dma_start(w_sc_rows[:, w].bitcast(I32), scales.rearrange("a q n -> q a n").bitcast(I32))
         load_wc(1)
         w_sc = keep.tile([P, 3, PASSES, N], U8, align_bytes=64)
-        nc.vector.memset(w_sc[:].rearrange("p w a n -> p (w a n)").bitcast(I32), 0)
         for r in range(4):
             nc.sync.dma_start(w_sc[r:P:32].rearrange("p w a n -> p (w a n)").bitcast(I32),
                               w_sc_rows[r:16:4].rearrange("p w a n -> p (w a n)").bitcast(I32))
@@ -69,8 +68,9 @@ def tile_list_rgg_ownsiluP_kernel(tc, tab_words, tab_scales, wa_words, wa_scales
 
         ident = keep.tile([P, P], F32)
         make_identity(nc, ident[:])
-        warm = keep.tile([P, 1], F32)
-        nc.scalar.activation(warm[:], ident[:, 0:1], ACT.Silu)
+        warm = keep.tile([P, 2], F32)
+        nc.vector.memset(warm[:, 0:1], 0.0)
+        nc.scalar.activation(warm[:, 1:2], warm[:, 0:1], ACT.Silu)
 
         got_sc = keep.tile([P, 2, J], U8, align_bytes=64)
         for side in (DST, SRC):
@@ -101,29 +101,31 @@ def tile_list_rgg_ownsiluP_kernel(tc, tab_words, tab_scales, wa_words, wa_scales
         def quantise_wc(a, half):
             cols = slice(half * N // 2, (half + 1) * N // 2)
             wc_bf = keep.tile([P, N // 2, 4], BF16, align_bytes=64, name="wc_bf", tag="stage%d" % (2 * a + half))
-            nc.scalar.copy(wc_bf[:].rearrange("p (t m) i -> p m i t", t=2), wc_raw[a, half])
+            nc.scalar.copy(wc_bf[:].rearrange("p (c k) i -> p c i k", k=4), wc_raw[a, half])
             nc.vector.quantize_mx(wc_w[:, a, cols].bitcast(FP8X4), wc_sc[:, a, cols], wc_bf[:].rearrange("p n i -> p (n i)"))
 
-        def gather_words(piece, tag):
+        def gather_words(piece, tags):
             first = piece * PIECE
-            got_w = keep.tile([P, 2, PIECE], U32, align_bytes=64, name="got_w", tag=tag)
+            got_w = {}
             for side in (DST, SRC):
-                nc.vector.tensor_copy(got_w[:, side, :],
+                got_w[side] = keep.tile([P, PIECE], U32, align_bytes=64, name="got_w", tag=tags[side])
+                nc.vector.tensor_copy(got_w[side][:],
                                       tab_w[:].bitcast(U32).indirect(lists[side][:, first // 16 : (first + PIECE) // 16]))
             parted = keep.tile([P, 2, PASSES, 2 * PIECE], U8, align_bytes=64, name="parted%d" % piece)
             for side in (DST, SRC):
-                nc.vector.tensor_copy(parted[:, side].bitcast(U16), got_w[:, side].bitcast(U16).rearrange("p (j a) -> p a j", a=2))
+                nc.vector.tensor_copy(parted[:, side].bitcast(U16), got_w[side][:].bitcast(U16).rearrange("p (j a) -> p a j", a=2))
             for j in range(first // P, (first + PIECE) // P):
                 node_w[j] = (parted, j * P - first)
 
         clear_page(0, "page0", nc.vector)
         clear_page(1, "page1", nc.vector)
-        gather_words(0, "got0")
-        for a in range(PASSES):
-            quantise_wc(a, 0)
-            quantise_wc(a, 1)
-        gather_words(1, "stage1")
-        gather_words(2, "stage3")
+        quantise_wc(0, 0)
+        quantise_wc(0, 1)
+        gather_words(0, ("got_src", "got_dst"))
+        gather_words(1, ("got_src", "got_dst"))
+        quantise_wc(1, 0)
+        quantise_wc(1, 1)
+        gather_words(2, ("stage3", "stage2"))
 
         owns = {}
         msgs = {}
@@ -194,12 +196,12 @@ def tile_list_rgg_ownsiluP_kernel(tc, tab_words, tab_scales, wa_words, wa_scales
             if j in GPSIMD_TILES:
                 plain = keep.tile([P, 4, P], F32, name="plain%d" % j)
                 for part in slices_of(j):
-                    nc.scalar.copy(plain[:, part], ms[:].rearrange("p (t m) -> p t m", t=4)[:, part])
+                    nc.scalar.copy(dealt(plain)[:, :, part], by_channel(ms)[:, :, part])
                 for part in slices_of(j):
                     nc.gpsimd.tensor_tensor(msg2[:, part], th[:, part], plain[:, part], ALU.mult)
                 msgs[j].append(plain)
             else:
-                nc.vector.scalar_tensor_tensor(msg2[:], th[:], 1.0, ms[:].rearrange("p (t m) -> p t m", t=4), ALU.add, ALU.mult)
+                nc.vector.scalar_tensor_tensor(msg2[:], th[:], 1.0, ms[:].rearrange("p (m t) -> p t m", t=4), ALU.add, ALU.mult)
 
         def turn(t, lo, hi, act):
             turned = psum.tile([P, 4, P], F32)
@@ -239,7 +241,7 @@ def tile_list_rgg_ownsiluP_kernel(tc, tab_words, tab_scales, wa_words, wa_scales
         combine(1)
         own_term(0)
         own_term(1)
-        gather_words(3, "th1")
+        gather_words(3, ("th1", "th0"))
         clear_page(2, "th1", nc.gpsimd)
         gate_sum(2)
         job(0, 0, 2, "act0_0")

@@ -37,10 +37,10 @@ def tile_list_rgg_ownsiluP_kernel(tc, tab_words, tab_scales, wa_words, wa_scales
         lists = [keep.tile([P, J // 16], U16, name="list_src"), keep.tile([P, J // 16], U16, name="list_dst")]
         tab_sc = keep.tile([P, T], U8, align_bytes=64, tag="early_late")
         nc.gpsimd.memset(tab_sc[:].bitcast(I32), 0)
-        nc.sync.dma_start(lists[DST][:], offs2)
         nc.sync.dma_start(lists[SRC][:], offs)
         for q in (0, 2, 1, 3):
             nc.sync.dma_start(tab_sc[32 * q : 32 * q + 8, :].bitcast(I32), tab_scales[:, 4 * q : 4 * q + 4, :].bitcast(I32))
+        nc.sync.dma_start(lists[DST][:], offs2)
         wc_rows = wc.rearrange("(a p i) n -> a p i n", a=PASSES, i=4)
         wc_raw = {}
 
@@ -53,14 +53,14 @@ def tile_list_rgg_ownsiluP_kernel(tc, tab_words, tab_scales, wa_words, wa_scales
         load_wc(0)
         tab_w = keep.tile([P, T], I32, align_bytes=64)
         nc.sync.dma_start(tab_w[:], tab_words[0].rearrange("p t i -> p (t i)").bitcast(I32))
-        w_sc_rows = keep.tile([16, 3, PASSES, N], U8, align_bytes=64)
+        w_sc_rows = keep.tile([32, 3, PASSES, N], U8, align_bytes=64)
         for w, scales in enumerate((wa_scales, wb_scales, wo_scales)):
-            nc.sync.dma_start(w_sc_rows[:, w].bitcast(I32), scales.rearrange("a q n -> q a n").bitcast(I32))
+            nc.sync.dma_start(w_sc_rows[16:32, w].bitcast(I32), scales.rearrange("a q n -> q a n").bitcast(I32))
         load_wc(1)
         w_sc = keep.tile([P, 3, PASSES, N], U8, align_bytes=64)
         for r in range(4):
             nc.sync.dma_start(w_sc[r:P:32].rearrange("p w a n -> p (w a n)").bitcast(I32),
-                              w_sc_rows[r:16:4].rearrange("p w a n -> p (w a n)").bitcast(I32))
+                              w_sc_rows[16 + r : 32 : 4].rearrange("p w a n -> p (w a n)").bitcast(I32))
         wa_w = keep.tile([P, PASSES, 2 * N], U8, align_bytes=64)
         nc.sync.dma_start(wa_w[:].bitcast(I32), wa_words.rearrange("a p c -> p a c").bitcast(I32))
         wb_w = keep.tile([P, PASSES, N], I32, align_bytes=64)
@@ -73,19 +73,21 @@ def tile_list_rgg_ownsiluP_kernel(tc, tab_words, tab_scales, wa_words, wa_scales
         nc.scalar.activation(warm[:, 1:2], warm[:, 0:1], ACT.Silu)
 
         got_sc = keep.tile([P, 2, J], U8, align_bytes=64)
-        for side in (DST, SRC):
+        for side in (SRC, DST):
             nc.vector.tensor_copy(got_sc[:, side, :], tab_sc[:].indirect(lists[side][:]))
-        got_sc1 = keep.tile([P, 2, J], U8, align_bytes=64, tag="early_late")
-        for r in range(4):
-            nc.sync.dma_start(got_sc1[r:P:32].rearrange("p l j -> p (l j)").bitcast(I32),
-                              got_sc[4 + r : P : 32].rearrange("p l j -> p (l j)").bitcast(I32))
-        wo_w = keep.tile([P, PASSES, 2 * N], U8, align_bytes=64)
-        nc.sync.dma_start(wo_w[:].bitcast(I32), wo_words.rearrange("a p c -> p a c").bitcast(I32))
-        gate_w = keep.tile([P, J], F32, tag="w_sc_rows", align_bytes=64)
-        nc.sync.dma_start(gate_w[:], wgo)
+        node_sc = {}
+
+        def move_scales(first, last, tag):
+            moved = keep.tile([P, 2, last - first], U8, align_bytes=64, name="moved", tag=tag)
+            for r in range(4):
+                nc.sync.dma_start(moved[r:P:32].bitcast(I32), got_sc[4 + r : P : 32, :, first:last].bitcast(I32))
+            for j in range(first // P, last // P):
+                node_sc[0, j] = got_sc[:, :, j * P : (j + 1) * P]
+                node_sc[1, j] = moved[:, :, j * P - first : (j + 1) * P - first]
+
+        move_scales(0, PIECE, "moved_first")
         bias = keep.tile([P, 4], F32)
         nc.sync.dma_start(bias[:], b.rearrange("(p t) -> p t", t=4))
-        node_sc = (got_sc, got_sc1)
 
         pages = {}
 
@@ -107,25 +109,31 @@ def tile_list_rgg_ownsiluP_kernel(tc, tab_words, tab_scales, wa_words, wa_scales
         def gather_words(piece, tags):
             first = piece * PIECE
             got_w = {}
-            for side in (DST, SRC):
+            for side in (SRC, DST):
                 got_w[side] = keep.tile([P, PIECE], U32, align_bytes=64, name="got_w", tag=tags[side])
                 nc.vector.tensor_copy(got_w[side][:],
                                       tab_w[:].bitcast(U32).indirect(lists[side][:, first // 16 : (first + PIECE) // 16]))
             parted = keep.tile([P, 2, PASSES, 2 * PIECE], U8, align_bytes=64, name="parted%d" % piece)
-            for side in (DST, SRC):
+            for side in (SRC, DST):
                 nc.vector.tensor_copy(parted[:, side].bitcast(U16), got_w[side][:].bitcast(U16).rearrange("p (j a) -> p a j", a=2))
             for j in range(first // P, (first + PIECE) // P):
                 node_w[j] = (parted, j * P - first)
 
         clear_page(0, "page0", nc.vector)
-        clear_page(1, "page1", nc.vector)
+        clear_page(1, "page1", nc.gpsimd)
+        clear_page(2, "page2", nc.gpsimd)
         quantise_wc(0, 0)
+        wo_w = keep.tile([P, PASSES, 2 * N], U8, align_bytes=64, tag="stage0")
+        nc.sync.dma_start(wo_w[:].bitcast(I32), wo_words.rearrange("a p c -> p a c").bitcast(I32))
         quantise_wc(0, 1)
+        move_scales(PIECE, J, "stage1")
         gather_words(0, ("got_src", "got_dst"))
         gather_words(1, ("got_src", "got_dst"))
+        gate_w = keep.tile([P, J], F32, tag="got_dst", align_bytes=64)
+        nc.sync.dma_start(gate_w[:], wgo)
         quantise_wc(1, 0)
         quantise_wc(1, 1)
-        gather_words(2, ("stage3", "stage2"))
+        gather_words(2, ("stage2", "stage3"))
 
         owns = {}
         msgs = {}
@@ -133,7 +141,7 @@ def tile_list_rgg_ownsiluP_kernel(tc, tab_words, tab_scales, wa_words, wa_scales
         def product(acc, j, side, a, w, w_scale, start, stop):
             parted, col = node_w[j]
             nc.tensor.matmul_mx(acc[:], lhsT=parted[:, side, a, 2 * col : 2 * col + 2 * P].bitcast(FP4X4),
-                                lhsT_scale=node_sc[a][:, side, j * P : (j + 1) * P],
+                                lhsT_scale=node_sc[a, j][:, side, :],
                                 rhs=w, rhs_scale=w_scale, start=start, stop=stop)
 
         def by_channel(bank):
@@ -229,7 +237,7 @@ def tile_list_rgg_ownsiluP_kernel(tc, tab_words, tab_scales, wa_words, wa_scales
 
         open_sums(0)
         open_sums(1)
-        for step in (target_pass, message_pass, source_pass):
+        for step in (message_pass, target_pass, source_pass):
             step(0, 0)
             step(1, 0)
         for j in (0, 1):
@@ -241,8 +249,7 @@ def tile_list_rgg_ownsiluP_kernel(tc, tab_words, tab_scales, wa_words, wa_scales
         combine(1)
         own_term(0)
         own_term(1)
-        gather_words(3, ("th1", "th0"))
-        clear_page(2, "th1", nc.gpsimd)
+        gather_words(3, ("th0", "th1"))
         gate_sum(2)
         job(0, 0, 2, "act0_0")
         clear_page(3, "act0_0", nc.gpsimd)

@@ -33,6 +33,7 @@ def tile_list_rgg_ownsiluP_kernel(tc, tab_words, tab_scales, wa_words, wa_scales
     with ExitStack() as ctx:
         keep = ctx.enter_context(tc.tile_pool(name="keep", bufs=1))
         psum = ctx.enter_context(tc.psum_pool(name="psum", bufs=2))
+        placed = ctx.enter_context(tc.tile_pool(name="placed", bufs=1))
 
         lists = [keep.tile([P, J // 16], U16, name="list_src"), keep.tile([P, J // 16], U16, name="list_dst")]
         tab_sc = keep.tile([P, T], U8, align_bytes=64, tag="early_late")
@@ -45,7 +46,7 @@ def tile_list_rgg_ownsiluP_kernel(tc, tab_words, tab_scales, wa_words, wa_scales
         wc_raw = {}
 
         def load_wc(a):
-            wc_pass = keep.tile([P, 4, N], F32, name="wc_pass%d" % a)
+            wc_pass = keep.tile([P, 4, N], F32, align_bytes=64, name="wc_pass", tag="wc_pass%d" % a)
             nc.sync.dma_start(wc_pass[:], wc_rows[a])
             for half in range(2):
                 wc_raw[a, half] = wc_pass[:].rearrange("p i (h c k) -> p h c i k", h=2, k=4)[:, half]
@@ -77,15 +78,14 @@ def tile_list_rgg_ownsiluP_kernel(tc, tab_words, tab_scales, wa_words, wa_scales
             nc.vector.tensor_copy(got_sc[:, side, :], tab_sc[:].indirect(lists[side][:]))
         node_sc = {}
 
-        def move_scales(first, last, tag):
-            moved = keep.tile([P, 2, last - first], U8, align_bytes=64, name="moved", tag=tag)
+        def move_scales(first, last, moved):
             for r in range(4):
                 nc.sync.dma_start(moved[r:P:32].bitcast(I32), got_sc[4 + r : P : 32, :, first:last].bitcast(I32))
             for j in range(first // P, last // P):
                 node_sc[0, j] = got_sc[:, :, j * P : (j + 1) * P]
                 node_sc[1, j] = moved[:, :, j * P - first : (j + 1) * P - first]
 
-        move_scales(0, PIECE, "moved_first")
+        move_scales(0, PIECE, keep.tile([P, 2, PIECE], U8, align_bytes=64, name="moved", tag="moved_first"))
         bias = keep.tile([P, 4], F32)
         nc.sync.dma_start(bias[:], b.rearrange("(p t) -> p t", t=4))
 
@@ -102,20 +102,27 @@ def tile_list_rgg_ownsiluP_kernel(tc, tab_words, tab_scales, wa_words, wa_scales
 
         def quantise_wc(a, half):
             cols = slice(half * N // 2, (half + 1) * N // 2)
-            wc_bf = keep.tile([P, N // 2, 4], BF16, align_bytes=64, name="wc_bf", tag="stage%d" % (2 * a + half))
+            if (a, half) == (0, 1):
+                wc_bf = placed.tile([P, N // 2, 4], BF16, align_bytes=64, name="wc_bf", offset=0)
+            else:
+                wc_bf = keep.tile([P, N // 2, 4], BF16, align_bytes=64, name="wc_bf", tag="stage%d" % (2 * a + half))
             nc.scalar.copy(wc_bf[:].rearrange("p (c k) i -> p c i k", k=4), wc_raw[a, half])
             nc.vector.quantize_mx(wc_w[:, a, cols].bitcast(FP8X4), wc_sc[:, a, cols], wc_bf[:].rearrange("p n i -> p (n i)"))
 
-        def gather_words(piece, tags):
+        def gather_side(piece, side, tag):
+            got_w = keep.tile([P, PIECE], U32, align_bytes=64, name="got_w", tag=tag)
+            columns = lists[side][:, piece * PIECE // 16 : (piece + 1) * PIECE // 16]
+            nc.vector.tensor_copy(got_w[:], tab_w[:].bitcast(U32).indirect(columns))
+            return got_w[:]
+
+        def gather_words(piece):
+            return [gather_side(piece, SRC, "got_src"), gather_side(piece, DST, "got_dst")]
+
+        def part_words(piece, got_w, tag):
             first = piece * PIECE
-            got_w = {}
+            parted = keep.tile([P, 2, PASSES, 2 * PIECE], U8, align_bytes=64, name="parted", tag=tag)
             for side in (SRC, DST):
-                got_w[side] = keep.tile([P, PIECE], U32, align_bytes=64, name="got_w", tag=tags[side])
-                nc.vector.tensor_copy(got_w[side][:],
-                                      tab_w[:].bitcast(U32).indirect(lists[side][:, first // 16 : (first + PIECE) // 16]))
-            parted = keep.tile([P, 2, PASSES, 2 * PIECE], U8, align_bytes=64, name="parted%d" % piece)
-            for side in (SRC, DST):
-                nc.vector.tensor_copy(parted[:, side].bitcast(U16), got_w[side][:].bitcast(U16).rearrange("p (j a) -> p a j", a=2))
+                nc.vector.tensor_copy(parted[:, side].bitcast(U16), got_w[side].bitcast(U16).rearrange("p (j a) -> p a j", a=2))
             for j in range(first // P, (first + PIECE) // P):
                 node_w[j] = (parted, j * P - first)
 
@@ -126,14 +133,16 @@ def tile_list_rgg_ownsiluP_kernel(tc, tab_words, tab_scales, wa_words, wa_scales
         wo_w = keep.tile([P, PASSES, 2 * N], U8, align_bytes=64, tag="stage0")
         nc.sync.dma_start(wo_w[:].bitcast(I32), wo_words.rearrange("a p c -> p a c").bitcast(I32))
         quantise_wc(0, 1)
-        move_scales(PIECE, J, "stage1")
-        gather_words(0, ("got_src", "got_dst"))
-        gather_words(1, ("got_src", "got_dst"))
-        gate_w = keep.tile([P, J], F32, tag="got_dst", align_bytes=64)
+        move_scales(PIECE, J, placed.tile([P, 2, J - PIECE], U8, align_bytes=64, name="moved_rest", offset=0))
+        gate_w = placed.tile([P, J], F32, align_bytes=64, offset=2 * (J - PIECE))
         nc.sync.dma_start(gate_w[:], wgo)
+        part_words(0, gather_words(0), "parted0")
+        part_words(1, gather_words(1), "parted1")
+        got_third = gather_words(2)
         quantise_wc(1, 0)
         quantise_wc(1, 1)
-        gather_words(2, ("stage2", "stage3"))
+        part_words(2, got_third, "wc_pass1")
+        last_src = gather_side(3, SRC, "got_src")
 
         owns = {}
         msgs = {}
@@ -243,17 +252,21 @@ def tile_list_rgg_ownsiluP_kernel(tc, tab_words, tab_scales, wa_words, wa_scales
         for j in (0, 1):
             target_pass(j, 1)
             source_pass(j, 1)
+        own_term(0)
         message_pass(0, 1)
         message_pass(1, 1)
         combine(0)
         combine(1)
-        own_term(0)
         own_term(1)
-        gather_words(3, ("th0", "th1"))
-        gate_sum(2)
+        part_words(3, [last_src, gather_side(3, DST, "moved_first")], "parted3")
+        open_sums(2)
+        target_pass(2, 0)
+        target_pass(2, 1)
         job(0, 0, 2, "act0_0")
         clear_page(3, "act0_0", nc.gpsimd)
         job(1, 0, 2, "act1_0")
+        source_pass(2, 0)
+        source_pass(2, 1)
         gated_message(2)
         gated_message(3)
         job(2, 0, 2, "act2_0")

@@ -142,7 +142,6 @@ def tile_list_rgg_ownsiluP_kernel(tc, tab_words, tab_scales, wa_words, wa_scales
         quantise_wc(1, 0)
         quantise_wc(1, 1)
         part_words(2, got_third, "wc_pass1")
-        last_src = gather_side(3, SRC, "got_src")
 
         owns = {}
         msgs = {}
@@ -220,29 +219,34 @@ def tile_list_rgg_ownsiluP_kernel(tc, tab_words, tab_scales, wa_words, wa_scales
             else:
                 nc.vector.scalar_tensor_tensor(msg2[:], th[:], 1.0, ms[:].rearrange("p (m t) -> p t m", t=4), ALU.add, ALU.mult)
 
-        def turn(t, lo, hi, act):
+        def turn(runs):
             turned = psum.tile([P, 4, P], F32)
-            for j in range(lo, hi):
-                terms = [owns[j]] + msgs[j][::-1]
-                for n, term in enumerate(terms):
-                    nc.tensor.matmul(turned[:, j - lo, :], lhsT=term[:, t, :], rhs=ident[:], start=n == 0, stop=n == len(terms) - 1,
-                                     is_transpose=True)
-            nc.scalar.activation(act, turned[:, 0 : hi - lo, :].rearrange("p j m -> p (j m)"),
-                                 ACT.Silu, bias=bias[:, t : t + 1], scale=0.5)
+            block = 0
+            for t, lo, hi in runs:
+                for j in range(lo, hi):
+                    terms = [owns[j]] + msgs[j][::-1]
+                    for n, term in enumerate(terms):
+                        nc.tensor.matmul(turned[:, block, :], lhsT=term[:, t, :], rhs=ident[:], start=n == 0, stop=n == len(terms) - 1,
+                                         is_transpose=True)
+                    block += 1
+            return turned
 
-        def job(t, lo, hi, tag, fused=True):
-            act = keep.tile([P, (hi - lo) * P], F32, align_bytes=64, name="act", tag=tag)
-            banks = -(-(hi - lo) // 4)
-            step = (hi - lo) // banks
-            for first in range(lo, hi, step):
-                turn(t, first, first + step, act[:, (first - lo) * P : (first - lo + step) * P])
-            window = pages[t][:].indirect(lists[DST][:, lo * 8 : hi * 8])
-            if fused:
-                nc.vector.tensor_tensor(window, act[:], gate_w[:, lo * P : hi * P], ALU.mult)
-            else:
-                weighted = keep.tile([P, (hi - lo) * P], F32, align_bytes=64, name="weighted%d_%d" % (t, lo))
-                nc.gpsimd.tensor_tensor(weighted[:], act[:], gate_w[:, lo * P : hi * P], ALU.mult)
-                nc.vector.tensor_copy(window, weighted[:])
+        def job(runs, fused=True, tags=None):
+            turned = turn(runs)
+            block = 0
+            for n, (t, lo, hi) in enumerate(runs):
+                tag = tags[n] if tags else "act%d_%d" % (t, lo)
+                act = keep.tile([P, (hi - lo) * P], F32, align_bytes=64, name="act", tag=tag)
+                nc.scalar.activation(act[:], turned[:, block : block + hi - lo, :].rearrange("p j m -> p (j m)"),
+                                     ACT.Silu, bias=bias[:, t : t + 1], scale=0.5)
+                block += hi - lo
+                window = pages[t][:].indirect(lists[DST][:, lo * 8 : hi * 8])
+                if fused:
+                    nc.vector.tensor_tensor(window, act[:], gate_w[:, lo * P : hi * P], ALU.mult)
+                else:
+                    weighted = keep.tile([P, (hi - lo) * P], F32, align_bytes=64, name="weighted%d_%d" % (t, lo))
+                    nc.gpsimd.tensor_tensor(weighted[:], act[:], gate_w[:, lo * P : hi * P], ALU.mult)
+                    nc.vector.tensor_copy(window, weighted[:])
 
         open_sums(0)
         open_sums(1)
@@ -258,39 +262,42 @@ def tile_list_rgg_ownsiluP_kernel(tc, tab_words, tab_scales, wa_words, wa_scales
         combine(0)
         combine(1)
         own_term(1)
-        part_words(3, [last_src, gather_side(3, DST, "moved_first")], "parted3")
+        part_words(3, [gather_side(3, SRC, "moved_first"), gather_side(3, DST, "parted0")], "parted3")
         open_sums(2)
         target_pass(2, 0)
         target_pass(2, 1)
-        job(0, 0, 2, "act0_0")
+        job([(0, 0, 2)])
         clear_page(3, "act0_0", nc.gpsimd)
-        job(1, 0, 2, "act1_0")
+        job([(1, 0, 2)])
         source_pass(2, 0)
         source_pass(2, 1)
         gated_message(2)
         gated_message(3)
-        job(2, 0, 2, "act2_0")
-        job(3, 0, 2, "act3_0")
+        job([(2, 0, 2)])
+        job([(3, 0, 2)])
         own_term(2)
         own_term(3)
         gated_message(4)
-        job(0, 2, 4, "act0_2", False)
-        job(1, 2, 4, "act1_2", False)
+        job([(0, 2, 4)], False)
+        job([(1, 2, 4), (2, 2, 4)], False)
         gated_message(5)
         own_term(4)
         own_term(5)
-        job(2, 2, 4, "act2_2", False)
-        job(0, 4, 6, "act0_4", False)
-        job(1, 4, 6, "act1_4", False)
+        open_sums(6)
+        target_pass(6, 0)
+        target_pass(6, 1)
+        job([(0, 4, 6)], False)
+        job([(1, 4, 6), (2, 4, 6)], False)
+        source_pass(6, 0)
+        source_pass(6, 1)
         gated_message(6)
-        job(2, 4, 6, "act2_4", False)
         gated_message(7)
         own_term(6)
         own_term(7)
-        job(0, 6, 8, "act0_6")
-        job(1, 6, 8, "act1_6")
-        job(2, 6, 8, "act2_6")
-        job(3, 2, 6, "act3_2")
+        job([(0, 6, 8)])
+        job([(1, 6, 8)])
+        job([(2, 6, 8)])
+        job([(3, 2, 6)])
 
         out_rows = out_0.rearrange("(p t) c -> p t c", t=4)
         for t in range(3):
@@ -328,7 +335,7 @@ def tile_list_rgg_ownsiluP_kernel(tc, tab_words, tab_scales, wa_words, wa_scales
         round_page(nc.scalar.copy, 1, va)
         round_page(nc.scalar.copy, 1, vb)
         round_page(nc.scalar.copy, 2, va)
-        job(3, 6, 8, "act2_6")
+        job([(3, 6, 8)], tags=["act2_6"])
         nc.sync.dma_start(out_rows[:, 3, :], pages[3][:])
         for t in (1, 2):
             for chunk in SCALAR_CHUNKS:

from contextlib import ExitStack

import concourse.mybir as mybir
from concourse.masks import make_identity

K, N, T, J = 1024, 512, 2048, 1024
FLOPS = 4 * 2 * K * N * J

F32 = mybir.dt.float32
BF16 = mybir.dt.bfloat16
I32 = mybir.dt.int32
U32 = mybir.dt.uint32
U16 = mybir.dt.uint16
U8 = mybir.dt.uint8
FP8X4 = mybir.dt.float8_e4m3fn_x4
FP4X4 = mybir.dt.float4_e2m1fn_x4
ACT = mybir.ActivationFunctionType
ALU = mybir.AluOpType

P = 128
PASSES = 2
EDGE_TILES = J // P
PIECE = 256
VECTOR_CHUNKS = ((0, 512), (512, 1024))
SCALAR_CHUNKS = ((1024, 1280), (1280, 1536), (1536, 1792), (1792, 2048))
SRC, DST = 0, 1
GPSIMD_TILES = (5, 6, 7)


def tile_list_rgg_ownsiluP_kernel(tc, tab_words, tab_scales, wa_words, wa_scales, wb_words, wb_scales, wc,
        wo_words, wo_scales, b, wgo, offs, offs2, out_0, out_1, out_2):
    nc = tc.nc
    with ExitStack() as ctx:
        keep = ctx.enter_context(tc.tile_pool(name="keep", bufs=1))
        psum = ctx.enter_context(tc.psum_pool(name="psum", bufs=2))
        placed = ctx.enter_context(tc.tile_pool(name="placed", bufs=1))

        lists = [keep.tile([P, J // 16], U16, name="list_src"), keep.tile([P, J // 16], U16, name="list_dst")]
        tab_sc = keep.tile([P, T], U8, align_bytes=64, tag="early_late")
        nc.gpsimd.memset(tab_sc[:].bitcast(I32), 0)
        nc.sync.dma_start(lists[SRC][:], offs)
        for q in (0, 2, 1, 3):
            nc.sync.dma_start(tab_sc[32 * q : 32 * q + 8, :].bitcast(I32), tab_scales[:, 4 * q : 4 * q + 4, :].bitcast(I32))
        nc.sync.dma_start(lists[DST][:], offs2)
        wc_rows = wc.rearrange("(a p i) n -> a p i n", a=PASSES, i=4)
        wc_raw = {}

        def load_wc(a):
            wc_pass = keep.tile([P, 4, N], F32, align_bytes=64, name="wc_pass", tag="wc_pass%d" % a)
            nc.sync.dma_start(wc_pass[:], wc_rows[a])
            for half in range(2):
                wc_raw[a, half] = wc_pass[:].rearrange("p i (h c k) -> p h c i k", h=2, k=4)[:, half]

        load_wc(0)
        tab_w = keep.tile([P, T], I32, align_bytes=64)
        nc.sync.dma_start(tab_w[:], tab_words[0].rearrange("p t i -> p (t i)").bitcast(I32))
        w_sc_rows = keep.tile([32, 3, PASSES, N], U8, align_bytes=64)
        for w, scales in enumerate((wa_scales, wb_scales, wo_scales)):
            nc.sync.dma_start(w_sc_rows[16:32, w].bitcast(I32), scales.rearrange("a q n -> q a n").bitcast(I32))
        load_wc(1)
        w_sc = keep.tile([P, 3, PASSES, N], U8, align_bytes=64)
        for r in range(4):
            nc.sync.dma_start(w_sc[r:P:32].rearrange("p w a n -> p (w a n)").bitcast(I32),
                              w_sc_rows[16 + r : 32 : 4].rearrange("p w a n -> p (w a n)").bitcast(I32))
        wa_w = keep.tile([P, PASSES, 2 * N], U8, align_bytes=64)
        nc.sync.dma_start(wa_w[:].bitcast(I32), wa_words.rearrange("a p c -> p a c").bitcast(I32))
        wb_w = keep.tile([P, PASSES, N], I32, align_bytes=64)
        nc.sync.dma_start(wb_w[:], wb_words.rearrange("a p n i -> p a (n i)").bitcast(I32))

        ident = keep.tile([P, P], F32)
        make_identity(nc, ident[:])
        warm = keep.tile([P, 2], F32)
        nc.vector.memset(warm[:, 0:1], 0.0)
        nc.scalar.activation(warm[:, 1:2], warm[:, 0:1], ACT.Silu)

        got_sc = keep.tile([P, 2, J], U8, align_bytes=64)
        for side in (SRC, DST):
            nc.vector.tensor_copy(got_sc[:, side, :], tab_sc[:].indirect(lists[side][:]))
        node_sc = {}

        def move_scales(first, last, moved):
            for r in range(4):
                nc.sync.dma_start(moved[r:P:32].bitcast(I32), got_sc[4 + r : P : 32, :, first:last].bitcast(I32))
            for j in range(first // P, last // P):
                node_sc[0, j] = got_sc[:, :, j * P : (j + 1) * P]
                node_sc[1, j] = moved[:, :, j * P - first : (j + 1) * P - first]

        move_scales(0, PIECE, keep.tile([P, 2, PIECE], U8, align_bytes=64, name="moved", tag="moved_first"))
        bias = keep.tile([P, 4], F32)
        nc.sync.dma_start(bias[:], b.rearrange("(p t) -> p t", t=4))

        pages = {}

        def clear_page(t, tag, engine):
            page = keep.tile([P, T], F32, align_bytes=64, name="page%d" % t, tag=tag)
            engine.memset(page[:].bitcast(I32), 0)
            pages[t] = page

        wc_w = keep.tile([P, PASSES, N], U32, align_bytes=64)
        wc_sc = keep.tile([P, PASSES, N], U8, align_bytes=64)
        node_w = {}

        def quantise_wc(a, half):
            cols = slice(half * N // 2, (half + 1) * N // 2)
            if (a, half) == (0, 1):
                wc_bf = placed.tile([P, N // 2, 4], BF16, align_bytes=64, name="wc_bf", offset=0)
            else:
                wc_bf = keep.tile([P, N // 2, 4], BF16, align_bytes=64, name="wc_bf", tag="stage%d" % (2 * a + half))
            nc.scalar.copy(wc_bf[:].rearrange("p (c k) i -> p c i k", k=4), wc_raw[a, half])
            nc.vector.quantize_mx(wc_w[:, a, cols].bitcast(FP8X4), wc_sc[:, a, cols], wc_bf[:].rearrange("p n i -> p (n i)"))

        def gather_side(piece, side, tag):
            got_w = keep.tile([P, PIECE], U32, align_bytes=64, name="got_w", tag=tag)
            columns = lists[side][:, piece * PIECE // 16 : (piece + 1) * PIECE // 16]
            nc.vector.tensor_copy(got_w[:], tab_w[:].bitcast(U32).indirect(columns))
            return got_w[:]

        def gather_words(piece):
            return [gather_side(piece, SRC, "got_src"), gather_side(piece, DST, "got_dst")]

        def part_words(piece, got_w, tag):
            first = piece * PIECE
            parted = keep.tile([P, 2, PASSES, 2 * PIECE], U8, align_bytes=64, name="parted", tag=tag)
            for side in (SRC, DST):
                nc.vector.tensor_copy(parted[:, side].bitcast(U16), got_w[side].bitcast(U16).rearrange("p (j a) -> p a j", a=2))
            for j in range(first // P, (first + PIECE) // P):
                node_w[j] = (parted, j * P - first)

        clear_page(0, "page0", nc.vector)
        clear_page(1, "page1", nc.gpsimd)
        clear_page(2, "page2", nc.gpsimd)
        quantise_wc(0, 0)
        wo_w = keep.tile([P, PASSES, 2 * N], U8, align_bytes=64, tag="stage0")
        nc.sync.dma_start(wo_w[:].bitcast(I32), wo_words.rearrange("a p c -> p a c").bitcast(I32))
        quantise_wc(0, 1)
        move_scales(PIECE, J, placed.tile([P, 2, J - PIECE], U8, align_bytes=64, name="moved_rest", offset=0))
        gate_w = placed.tile([P, J], F32, align_bytes=64, offset=2 * (J - PIECE))
        nc.sync.dma_start(gate_w[:], wgo)
        part_words(0, gather_words(0), "parted0")
        part_words(1, gather_words(1), "parted1")
        got_third = gather_words(2)
        quantise_wc(1, 0)
        quantise_wc(1, 1)
        part_words(2, got_third, "wc_pass1")

        owns = {}
        msgs = {}

        def product(acc, j, side, a, w, w_scale, start, stop):
            parted, col = node_w[j]
            nc.tensor.matmul_mx(acc[:], lhsT=parted[:, side, a, 2 * col : 2 * col + 2 * P].bitcast(FP4X4),
                                lhsT_scale=node_sc[a, j][:, side, :],
                                rhs=w, rhs_scale=w_scale, start=start, stop=stop)

        def by_channel(bank):
            return bank[:].rearrange("p (m t) -> p m t", t=4)

        def dealt(tile):
            return tile[:].rearrange("p t m -> p m t")

        def slices_of(j):
            return (slice(0, 1), slice(1, 4)) if j in GPSIMD_TILES and j % 2 else (slice(0, 4),)

        sums = {}

        def open_sums(j):
            za = psum.tile([P, N], F32)
            ms = psum.tile([P, N], F32)
            sums[j] = (za, ms)

        def target_pass(j, a):
            product(sums[j][0], j, DST, a, wa_w[:, a, :].bitcast(FP4X4), w_sc[:, 0, a, :], a == 0, False)

        def source_pass(j, a):
            product(sums[j][0], j, SRC, a, wb_w[:, a, :].bitcast(FP8X4), w_sc[:, 1, a, :], False, a == PASSES - 1)

        def message_pass(j, a):
            product(sums[j][1], j, SRC, a, wc_w[:, a, :].bitcast(FP8X4), wc_sc[:, a, :], a == 0, a == PASSES - 1)

        def own_term(j):
            ow = psum.tile([P, N], F32)
            for a in range(PASSES):
                product(ow, j, DST, a, wo_w[:, a, :].bitcast(FP4X4), w_sc[:, 2, a, :], a == 0, a == PASSES - 1)
            own2 = keep.tile([P, 4, P], F32, align_bytes=64, name="own", tag="own%d" % j)
            for part in slices_of(j):
                nc.scalar.activation(dealt(own2)[:, :, part], by_channel(ow)[:, :, part], ACT.Copy, scale=2.0)
            owns[j] = own2

        def gate_sum(j):
            open_sums(j)
            for a in range(PASSES):
                target_pass(j, a)
                source_pass(j, a)

        def gated_message(j):
            if j not in sums:
                gate_sum(j)
            for a in range(PASSES):
                message_pass(j, a)
            combine(j)

        def multiply(j):
            gated_message(j)
            own_term(j)

        def combine(j):
            za, ms = sums[j]
            th = keep.tile([P, 4, P], F32, align_bytes=64, name="th", tag="th%d" % j)
            nc.scalar.activation(dealt(th), by_channel(za), ACT.Tanh, scale=0.5)
            msg2 = keep.tile([P, 4, P], F32, align_bytes=64, name="msg", tag="msg%d" % j)
            msgs[j] = [msg2]
            if j in GPSIMD_TILES:
                plain = keep.tile([P, 4, P], F32, name="plain%d" % j)
                for part in slices_of(j):
                    nc.scalar.copy(dealt(plain)[:, :, part], by_channel(ms)[:, :, part])
                for part in slices_of(j):
                    nc.gpsimd.tensor_tensor(msg2[:, part], th[:, part], plain[:, part], ALU.mult)
                msgs[j].append(plain)
            else:
                nc.vector.scalar_tensor_tensor(msg2[:], th[:], 1.0, ms[:].rearrange("p (m t) -> p t m", t=4), ALU.add, ALU.mult)

        def turn(runs):
            turned = psum.tile([P, 4, P], F32)
            block = 0
            for t, lo, hi in runs:
                for j in range(lo, hi):
                    terms = [owns[j]] + msgs[j][::-1]
                    for n, term in enumerate(terms):
                        nc.tensor.matmul(turned[:, block, :], lhsT=term[:, t, :], rhs=ident[:], start=n == 0, stop=n == len(terms) - 1,
                                         is_transpose=True)
                    block += 1
            return turned

        def job(runs, fused=True, tags=None):
            turned = turn(runs)
            block = 0
            for n, (t, lo, hi) in enumerate(runs):
                tag = tags[n] if tags else "act%d_%d" % (t, lo)
                act = keep.tile([P, (hi - lo) * P], F32, align_bytes=64, name="act", tag=tag)
                nc.scalar.activation(act[:], turned[:, block : block + hi - lo, :].rearrange("p j m -> p (j m)"),
                                     ACT.Silu, bias=bias[:, t : t + 1], scale=0.5)
                block += hi - lo
                window = pages[t][:].indirect(lists[DST][:, lo * 8 : hi * 8])
                if fused:
                    nc.vector.tensor_tensor(window, act[:], gate_w[:, lo * P : hi * P], ALU.mult)
                else:
                    weighted = keep.tile([P, (hi - lo) * P], F32, align_bytes=64, name="weighted%d_%d" % (t, lo))
                    nc.gpsimd.tensor_tensor(weighted[:], act[:], gate_w[:, lo * P : hi * P], ALU.mult)
                    nc.vector.tensor_copy(window, weighted[:])

        open_sums(0)
        open_sums(1)
        for step in (message_pass, target_pass, source_pass):
            step(0, 0)
            step(1, 0)
        for j in (0, 1):
            target_pass(j, 1)
            source_pass(j, 1)
        own_term(0)
        message_pass(0, 1)
        message_pass(1, 1)
        combine(0)
        combine(1)
        own_term(1)
        part_words(3, [gather_side(3, SRC, "moved_first"), gather_side(3, DST, "parted0")], "parted3")
        open_sums(2)
        target_pass(2, 0)
        target_pass(2, 1)
        job([(0, 0, 2)])
        clear_page(3, "act0_0", nc.gpsimd)
        job([(1, 0, 2)])
        source_pass(2, 0)
        source_pass(2, 1)
        gated_message(2)
        gated_message(3)
        job([(2, 0, 2)])
        job([(3, 0, 2)])
        own_term(2)
        own_term(3)
        gated_message(4)
        job([(0, 2, 4)], False)
        job([(1, 2, 4), (2, 2, 4)], False)
        gated_message(5)
        own_term(4)
        own_term(5)
        open_sums(6)
        target_pass(6, 0)
        target_pass(6, 1)
        job([(0, 4, 6)], False)
        job([(1, 4, 6), (2, 4, 6)], False)
        source_pass(6, 0)
        source_pass(6, 1)
        gated_message(6)
        gated_message(7)
        own_term(6)
        own_term(7)
        job([(0, 6, 8)])
        job([(1, 6, 8)])
        job([(2, 6, 8)])
        job([(3, 2, 6)])

        out_rows = out_0.rearrange("(p t) c -> p t c", t=4)
        for t in range(3):
            nc.sync.dma_start(out_rows[:, t, :], pages[t][:])

        pairs = {}
        woven = {}
        for chunk, tag in zip(VECTOR_CHUNKS + SCALAR_CHUNKS, ("msg5", "own5", "msg4", "own4", "msg3", "own3")):
            lo, hi = chunk
            pairs[chunk] = keep.tile([P, 2, hi - lo, 2], BF16, align_bytes=64, name="pairs", tag=tag)
            woven[chunk] = keep.tile([P, hi - lo, 4], BF16, align_bytes=64, name="woven%d" % lo)
        codes = keep.tile([P, T], U32, align_bytes=64)
        code_sc = keep.tile([P, T // 2], U8, align_bytes=64)
        out_words = out_1[0].rearrange("p t i -> p (t i)").bitcast(I32)

        def round_page(copy, t, chunk):
            copy(pairs[chunk][:, t // 2, :, t % 2], pages[t][:, chunk[0] : chunk[1]])

        def weave(copy, chunk):
            words = pairs[chunk][:].rearrange("p h c e -> p h (c e)").bitcast(F32)
            copy(woven[chunk][:].bitcast(F32), words.rearrange("p h c -> p c h"))

        def quantise(chunk):
            cols = slice(chunk[0], chunk[1])
            half, first = divmod(chunk[0], T // 2)
            plane = code_sc[4 * half :, first : first + chunk[1] - chunk[0]]
            nc.vector.quantize_mx(codes[:, cols].bitcast(FP8X4), plane, woven[chunk][:].rearrange("p c i -> p (c i)"))

        def store_codes(lo, hi):
            nc.sync.dma_start(out_words[:, lo:hi], codes[:, lo:hi].bitcast(I32))

        for chunk in VECTOR_CHUNKS + SCALAR_CHUNKS:
            round_page(nc.scalar.copy, 0, chunk)
        va, vb = VECTOR_CHUNKS
        round_page(nc.scalar.copy, 1, va)
        round_page(nc.scalar.copy, 1, vb)
        round_page(nc.scalar.copy, 2, va)
        job([(3, 6, 8)], tags=["act2_6"])
        nc.sync.dma_start(out_rows[:, 3, :], pages[3][:])
        for t in (1, 2):
            for chunk in SCALAR_CHUNKS:
                round_page(nc.scalar.copy, t, chunk)
        for chunk in SCALAR_CHUNKS:
            round_page(nc.scalar.copy, 3, chunk)
            weave(nc.scalar.copy, chunk)
        s0, s1, s2, s3 = SCALAR_CHUNKS
        vcopy = nc.vector.tensor_copy
        round_page(vcopy, 3, va)
        round_page(vcopy, 2, vb)
        weave(vcopy, va)
        round_page(vcopy, 3, vb)
        quantise(va)
        weave(vcopy, vb)
        quantise(s0)
        quantise(vb)
        store_codes(va[0], vb[1])
        quantise(s1)
        store_codes(s0[0], s1[1])
        quantise(s2)
        store_codes(s2[0], s2[1])
        quantise(s3)
        store_codes(s3[0], s3[1])
        for q in (0, 2, 1, 3):
            queue = nc.scalar if q < 3 else nc.sync
            rows = out_2[0, 4 * q : 4 * q + 4, :].rearrange("r (h c) -> h r c", h=2)
            queue.dma_start(rows.bitcast(I32), code_sc[32 * q : 32 * q + 8, :].bitcast(I32))
